import numpy as np
import ml_dtypes


def mxq(x, axis, fmt="e4m3"):
    dtype, down = {"e4m3": (ml_dtypes.float8_e4m3fn, 7), "e5m2": (ml_dtypes.float8_e5m2, 14)}[fmt]
    v = np.moveaxis(np.asarray(x, np.float32).astype(ml_dtypes.bfloat16).astype(np.float64), axis, -1)
    blocks = v.reshape(v.shape[:-1] + (-1, 32))
    amax = np.abs(blocks).max(-1, keepdims=True)
    byte = np.maximum(np.where(amax > 0, np.frexp(amax)[1] - 1 + 127, 0) - down, 1)
    scale = np.exp2(byte - 127.0)
    codes = (blocks / scale).astype(np.float32).astype(dtype).astype(np.float64)
    return np.moveaxis((codes * scale).reshape(v.shape), -1, axis)


WIDE = False


def mx_kscale(k):
    if not WIDE:
        return np.ones(k)
    levels = np.array([10, -10, 5, -5, 0])
    if k % 512:
        return np.exp2(np.random.permutation(np.resize(levels, k // 32))).repeat(32)
    a = np.empty((k // 512, 16))
    for p in range(k // 512):
        a[p, :8] = np.random.permutation(np.resize(levels, 8))
        for g in range(8):
            far = levels[np.abs(levels - a[p, g]) >= 10]
            a[p, g + 8] = far[np.random.randint(len(far))]
    return np.exp2(a.ravel()).repeat(32)


def f64(x):
    return np.asarray(x).astype(np.float64)


def striped(idx):
    return np.tile(np.asarray(idx).reshape(-1, 16).T, (8, 1)).astype(np.uint16)


def unstriped(offs):
    return offs[:16].T.reshape(-1).astype(np.int64)


E2M1 = np.array([0.0, 0.5, 1.0, 1.5, 2.0, 3.0, 4.0, 6.0, -0.0, -0.5, -1.0, -1.5, -2.0, -3.0, -4.0, -6.0])


def pack_weight(w, fmt):
    k, n = w.shape
    w = f64(np.asarray(w, np.float32).astype(ml_dtypes.bfloat16)).reshape(k // 32, 32, n)
    amax = np.abs(w).max(1)
    if fmt == "e4m3":
        byte = np.frexp(amax)[1] - 1 + 127 - 7
    else:
        mant, ex = np.frexp(amax / 6.0)
        byte = np.where(mant > 0.5, ex, ex - 1) + 127
    byte = np.clip(np.where(amax > 0, byte, 1), 1, 254)
    scaled = (w * np.exp2(127.0 - byte)[:, None, :]).reshape(k, n).astype(np.float32)
    by_word = np.ascontiguousarray(scaled.reshape(k // 512, 128, 4, n).transpose(0, 1, 3, 2))
    if fmt == "e4m3":
        words = by_word.astype(ml_dtypes.float8_e4m3fn).view(np.uint8)
    else:
        c = by_word.astype(ml_dtypes.float4_e2m1fn).view(np.uint8) & 0xF
        words = (c[..., 0::2] | (c[..., 1::2] << 4)).reshape(k // 512, 128, 2 * n)
    return np.ascontiguousarray(words), np.ascontiguousarray(byte.astype(np.uint8).reshape(k // 512, 16, n))


def unpack_weight(words, scales, fmt):
    g, _, n = scales.shape
    words = np.ascontiguousarray(words).reshape(g, 128, n, -1)
    if fmt == "e4m3":
        vals = words.view(ml_dtypes.float8_e4m3fn).astype(np.float64)
    else:
        nib = np.empty((g, 128, n, 4), np.uint8)
        nib[..., 0::2] = words & 0xF
        nib[..., 1::2] = words >> 4
        vals = E2M1[nib]
    vals = vals * np.repeat(np.exp2(scales.astype(np.float64) - 127.0), 8, axis=1)[..., None]
    return vals.transpose(0, 1, 3, 2).reshape(g * 512, n)


B, N, T, D, DV, NQ = 1, 512, 2048, 1024, 256, 128


def setup_inputs():
    n = np.random.standard_normal
    idx = np.random.permutation(T)[:B * N]
    s = mx_kscale(D)[:, None]
    u = np.ones(T)
    u[idx] = mx_kscale(B * N)
    r = np.random.uniform(0.5, 2.0, T)
    k = n((D, T)) / s
    v = n((DV, T)) / (u * r)
    kp = pack_weight(k, "e2m1")
    return {
        "qT": (n((B, D, NQ)) * s * (1.00 / np.sqrt(D))).astype(np.float32),
        "k_words": np.ascontiguousarray(kp[0].reshape(D // 1024, 2, 128, T, 2).transpose(0, 2, 3, 1, 4)).reshape(D // 1024, 128, T, 4),
        "k_scales": kp[1],
        "vT": v.astype(np.float32),
        "vs": np.tile(u * r, (128, 1)).astype(np.float32),
        "offs": striped(idx),
    }


def reference(qT, k_words, k_scales, vT, vs, offs):
    idx = unstriped(offs)
    k = unpack_weight(k_words.reshape(D // 1024, 128, T, 2, 2).transpose(0, 3, 1, 2, 4).reshape(D // 512, 128, 2 * T), k_scales, "e2m1")
    v = f64(vT)
    pick = lambda x: x[:, idx].reshape(x.shape[0], B, N).transpose(1, 0, 2)
    q = f64(qT)
    score = mxq(q, 1, "e4m3").transpose(0, 2, 1) @ pick(k)
    m = score.max(-1, keepdims=True)
    p = np.exp(score - m)
    total = p.sum(-1, keepdims=True)
    w = p * pick(f64(vs))[:, :1, :]
    y = mxq(w, 2, "e4m3") @ mxq(pick(v).transpose(0, 2, 1), 1, "e4m3")
    y = y / total
    return y

@@ -1,0 +1,162 @@
+from contextlib import ExitStack
+
+import concourse.mybir as mybir
+
+F32 = mybir.dt.float32
+BF16 = mybir.dt.bfloat16
+I32 = mybir.dt.int32
+U32 = mybir.dt.uint32
+U16 = mybir.dt.uint16
+U8 = mybir.dt.uint8
+FP8X4 = mybir.dt.float8_e4m3fn_x4
+FP4X4 = mybir.dt.float4_e2m1fn_x4
+ACT = mybir.ActivationFunctionType
+ALU = mybir.AluOpType
+AXIS = mybir.AxisListType
+
+P = 128
+PACK = 4
+N, T, D, DV, NQ = 512, 2048, 1024, 256, 128
+PASSES = D // (P * PACK)
+V_BLOCKS = DV // P
+VS_ROW = 8
+
+FLOPS = 2 * NQ * N * (D + DV)
+
+
+def tile_attend_soft_topk_kernel(tc, qT, k_words, k_scales, vT, vs, offs, out):
+    nc = tc.nc
+    with ExitStack() as ctx:
+        sb = ctx.enter_context(tc.tile_pool(name="sb", bufs=1))
+        ps = ctx.enter_context(tc.psum_pool(name="ps", bufs=1))
+
+        offsets = sb.tile([P, N // 16], U16, name="offsets")
+        key_pool = sb.tile([P, T], I32, name="key_pool", align_bytes=64)
+        scale_pool = sb.tile([P, PASSES, T], U8, name="scale_pool", align_bytes=64)
+        vs_pool = sb.tile([P, T], F32, name="vs_pool", align_bytes=64)
+        identity = sb.tile([P, P], F32, name="identity", align_bytes=64)
+        tags = ("q_slot", "v_slot")
+        zeros = [sb.tile([P, P // 2], F32, name=f"zeros{h}", tag=tags[h], align_bytes=64) for h in range(2)]
+        warm_out = sb.tile([P, 8], F32, name="warm_out")
+
+        nc.vector.memset(scale_pool[:].rearrange("p o t -> p (o t)").bitcast(I32), 0)
+        for h in range(2):
+            nc.vector.memset(zeros[h][:], 0.0)
+        nc.vector.memset(vs_pool[:], 0.0)
+        for h in range(2):
+            nc.gpsimd.affine_select(
+                out=identity[:, h * 64 : (h + 1) * 64],
+                in_=zeros[h][:],
+                compare_op=ALU.not_equal,
+                fill=1.0,
+                base=-64 * h,
+                pattern=[[-1, 64]],
+                channel_multiplier=1,
+            )
+        q_raw = sb.tile([P, PASSES, PACK, NQ], F32, name="q_raw", tag=tags[0], align_bytes=64)
+        v_pool = sb.tile([P, V_BLOCKS, T], F32, name="v_pool", tag=tags[1], align_bytes=64)
+
+        nc.sync.dma_start(offsets[:], offs)
+        nc.sync.dma_start(key_pool[:], k_words[0].rearrange("p t b -> p (t b)").bitcast(I32))
+        for quad in range(4):
+            nc.scalar.dma_start(
+                scale_pool[32 * quad : 32 * quad + 4, :, :].bitcast(I32),
+                k_scales[:, 4 * quad : 4 * quad + 4, :].rearrange("o f t -> f o t").bitcast(I32),
+            )
+        nc.sync.dma_start(q_raw[:], qT[0].rearrange("(o p j) q -> p o j q", o=PASSES, j=PACK))
+        for h in range(V_BLOCKS):
+            nc.sync.dma_start(v_pool[:, h, :], vT[h * P : (h + 1) * P, :])
+        nc.scalar.dma_start(vs_pool[VS_ROW : VS_ROW + 1, :], vs[0:1, :])
+        nc.scalar.activation(warm_out[:], identity[:, 0:8], ACT.Exp)
+
+        key_scales = sb.tile([P, PASSES, N], U8, name="key_scales", align_bytes=64)
+        key_pairs = sb.tile([P, N], U32, name="key_pairs", align_bytes=64)
+        key_words = sb.tile([P, PASSES, 2 * N], U8, name="key_words", align_bytes=64)
+        nc.vector.tensor_copy(key_pairs[:], key_pool[:].bitcast(U32).indirect(offsets[:]))
+        nc.vector.tensor_copy(key_scales[:, 0, :], scale_pool[:, 0, :].indirect(offsets[:]))
+        halves = key_pairs[:].bitcast(U16).rearrange("p (i o) -> p o i", o=PASSES)
+        for o in range(PASSES):
+            nc.vector.tensor_copy(key_words[:, o, :].bitcast(U16), halves[:, o, :])
+
+        q_bf = sb.tile([P, PASSES, NQ, PACK], BF16, name="q_bf", align_bytes=64)
+        q_codes = sb.tile([P, PASSES * NQ], U32, name="q_codes", align_bytes=64)
+        q_scales = sb.tile([P, PASSES * NQ], U8, name="q_scales", align_bytes=64)
+        for o in range(PASSES):
+            nc.scalar.activation(q_bf[:, o, :, :], q_raw[:, o, :, :].rearrange("p j q -> p q j"), ACT.Copy)
+        nc.vector.quantize_mx(q_codes[:].bitcast(FP8X4), q_scales[:], q_bf[:].rearrange("p o q j -> p (o q j)"))
+        nc.vector.tensor_copy(key_scales[:, 1, :], scale_pool[:, 1, :].indirect(offsets[:]))
+
+        scores = ps.tile([P, N], F32, name="scores")
+        for o in range(PASSES):
+            nc.tensor.matmul_mx(
+                scores[:],
+                lhsT=q_codes[:, o * NQ : (o + 1) * NQ].bitcast(FP8X4),
+                lhsT_scale=q_scales[:, o * NQ : (o + 1) * NQ],
+                rhs=key_words[:, o, :].bitcast(FP4X4),
+                rhs_scale=key_scales[:, o, :],
+                start=(o == 0),
+                stop=(o == PASSES - 1),
+            )
+
+        vs_listed = sb.tile([P, N], F32, name="vs_listed", align_bytes=64)
+        vs_turned = ps.tile([P, PACK, P], F32, name="vs_turned")
+        vs_slot = sb.tile([P, PACK], F32, name="vs_slot")
+        nc.vector.tensor_copy(vs_listed[:], vs_pool[:].indirect(offsets[:]))
+        for t in range(PACK):
+            nc.tensor.transpose(vs_turned[:, t, :], vs_listed[:, t::PACK], identity[:])
+        nc.scalar.activation(vs_slot[:], vs_turned[:, :, VS_ROW], ACT.Copy)
+
+        neg_max = sb.tile([P, 1], F32, name="neg_max")
+        total = sb.tile([P, 1], F32, name="total")
+        inv_total = sb.tile([P, 1], F32, name="inv_total")
+        probs = sb.tile([P, PACK, P], F32, name="probs", align_bytes=64)
+        nc.vector.tensor_reduce(neg_max[:], scores[:], AXIS.X, ALU.max, negate=True)
+        nc.scalar.activation(
+            probs[:], scores[:].rearrange("q (s t) -> q t s", t=PACK), ACT.Exp, bias=neg_max[:], accum_out=total[:]
+        )
+        probs_turned = ps.tile([P, PACK, NQ], F32, name="probs_turned")
+        for t in range(PACK):
+            nc.tensor.transpose(probs_turned[:, t, :], probs[:, t, :], identity[:])
+
+        v_codes = sb.tile([P, DV], U32, name="v_codes", align_bytes=64)
+        v_scales = sb.tile([P, DV], U8, name="v_scales", align_bytes=64)
+        v_bf = []
+        for h in range(V_BLOCKS):
+            v_listed = sb.tile([P, N], F32, name=f"v_listed{h}", align_bytes=64)
+            v_turned = ps.tile([P, PACK, P], F32, name=f"v_turned{h}")
+            v_bf.append(sb.tile([P, P, PACK], BF16, name=f"v_bf{h}", align_bytes=64))
+            nc.vector.tensor_copy(v_listed[:], v_pool[:, h, :].indirect(offsets[:]))
+            for t in range(PACK):
+                nc.tensor.transpose(v_turned[:, t, :], v_listed[:, t::PACK], identity[:])
+            nc.scalar.activation(v_bf[h][:], v_turned[:].rearrange("p t e -> p e t"), ACT.Copy)
+
+        w_bf = sb.tile([P, NQ, PACK], BF16, name="w_bf", align_bytes=64)
+        w_codes = sb.tile([P, NQ], U32, name="w_codes", align_bytes=64)
+        w_scales = sb.tile([P, NQ], U8, name="w_scales", align_bytes=64)
+        nc.vector.tensor_tensor(
+            w_bf[:],
+            probs_turned[:].rearrange("p t q -> p q t"),
+            vs_slot[:].unsqueeze(1).to_broadcast([P, NQ, PACK]),
+            ALU.mult,
+        )
+        nc.vector.reciprocal(inv_total[:], total[:])
+        nc.vector.quantize_mx(w_codes[:].bitcast(FP8X4), w_scales[:], w_bf[:].rearrange("p q t -> p (q t)"))
+
+        for h in range(V_BLOCKS):
+            cols = slice(h * P, (h + 1) * P)
+            nc.vector.quantize_mx(
+                v_codes[:, cols].bitcast(FP8X4), v_scales[:, cols], v_bf[h][:].rearrange("p e t -> p (e t)")
+            )
+            sums = ps.tile([P, P], F32, name=f"sums{h}")
+            result = sb.tile([P, P], F32, name=f"result{h}")
+            nc.tensor.matmul_mx(
+                sums[:],
+                lhsT=w_codes[:].bitcast(FP8X4),
+                lhsT_scale=w_scales[:],
+                rhs=v_codes[:, cols].bitcast(FP8X4),
+                rhs_scale=v_scales[:, cols],
+                start=True,
+                stop=True,
+            )
+            nc.scalar.activation(result[:], sums[:], ACT.Copy, scale=inv_total[:])
+            nc.sync.dma_start(out[0][:, cols], result[:])

@@ -1,6 +1,7 @@
 from contextlib import ExitStack
 
 import concourse.mybir as mybir
+from concourse.masks import make_identity
 
 F32 = mybir.dt.float32
 BF16 = mybir.dt.bfloat16
@@ -28,55 +29,46 @@ def tile_attend_soft_topk_kernel(tc, qT, k_words, k_scales, vT, vs, offs, out):
     nc = tc.nc
     with ExitStack() as ctx:
         sb = ctx.enter_context(tc.tile_pool(name="sb", bufs=1))
+        late = ctx.enter_context(tc.tile_pool(name="late", bufs=1))
         ps = ctx.enter_context(tc.psum_pool(name="ps", bufs=1))
 
         offsets = sb.tile([P, N // 16], U16, name="offsets")
         key_pool = sb.tile([P, T], I32, name="key_pool", align_bytes=64)
         scale_pool = sb.tile([P, PASSES, T], U8, name="scale_pool", align_bytes=64)
-        vs_pool = sb.tile([P, T], F32, name="vs_pool", align_bytes=64)
+        vs_pool = sb.tile([P, T], F32, name="vs_pool", tag="m_slot", align_bytes=64)
         identity = sb.tile([P, P], F32, name="identity", align_bytes=64)
-        tags = ("q_slot", "v_slot")
-        zeros = [sb.tile([P, P // 2], F32, name=f"zeros{h}", tag=tags[h], align_bytes=64) for h in range(2)]
         warm_out = sb.tile([P, 8], F32, name="warm_out")
 
-        nc.vector.memset(scale_pool[:].rearrange("p o t -> p (o t)").bitcast(I32), 0)
-        for h in range(2):
-            nc.vector.memset(zeros[h][:], 0.0)
+        nc.gpsimd.memset(scale_pool[:, 0, :].bitcast(I32), 0)
+        nc.vector.memset(scale_pool[:, 1, :].bitcast(I32), 0)
         nc.vector.memset(vs_pool[:], 0.0)
-        for h in range(2):
-            nc.gpsimd.affine_select(
-                out=identity[:, h * 64 : (h + 1) * 64],
-                in_=zeros[h][:],
-                compare_op=ALU.not_equal,
-                fill=1.0,
-                base=-64 * h,
-                pattern=[[-1, 64]],
-                channel_multiplier=1,
-            )
-        q_raw = sb.tile([P, PASSES, PACK, NQ], F32, name="q_raw", tag=tags[0], align_bytes=64)
-        v_pool = sb.tile([P, V_BLOCKS, T], F32, name="v_pool", tag=tags[1], align_bytes=64)
+        make_identity(nc, identity[:])
+        q_raw = sb.tile([P, PASSES, PACK, NQ], F32, name="q_raw", align_bytes=64)
+        v_pool = late.tile([P, V_BLOCKS, T], F32, name="v_pool", align_bytes=64, offset=0)
 
+        nc.scalar.activation(warm_out[:], identity[:, 0:8], ACT.Exp)
         nc.sync.dma_start(offsets[:], offs)
-        nc.sync.dma_start(key_pool[:], k_words[0].rearrange("p t b -> p (t b)").bitcast(I32))
+        q_rows = qT[0].rearrange("(o p j) q -> o p j q", o=PASSES, j=PACK)
+        nc.sync.dma_start(q_raw[:, 0, :, :], q_rows[0])
         for quad in range(4):
-            nc.scalar.dma_start(
+            nc.sync.dma_start(
                 scale_pool[32 * quad : 32 * quad + 4, :, :].bitcast(I32),
                 k_scales[:, 4 * quad : 4 * quad + 4, :].rearrange("o f t -> f o t").bitcast(I32),
             )
-        nc.sync.dma_start(q_raw[:], qT[0].rearrange("(o p j) q -> p o j q", o=PASSES, j=PACK))
+        nc.sync.dma_start(key_pool[:], k_words[0].rearrange("p t b -> p (t b)").bitcast(I32))
+        nc.sync.dma_start(q_raw[:, 1, :, :], q_rows[1])
+        nc.sync.dma_start(vs_pool[VS_ROW : VS_ROW + 1, :], vs[0:1, :])
         for h in range(V_BLOCKS):
             nc.sync.dma_start(v_pool[:, h, :], vT[h * P : (h + 1) * P, :])
-        nc.scalar.dma_start(vs_pool[VS_ROW : VS_ROW + 1, :], vs[0:1, :])
-        nc.scalar.activation(warm_out[:], identity[:, 0:8], ACT.Exp)
 
         key_scales = sb.tile([P, PASSES, N], U8, name="key_scales", align_bytes=64)
+        for o in range(PASSES):
+            nc.vector.tensor_copy(key_scales[:, o, :], scale_pool[:, o, :].indirect(offsets[:]))
+
         key_pairs = sb.tile([P, N], U32, name="key_pairs", align_bytes=64)
         key_words = sb.tile([P, PASSES, 2 * N], U8, name="key_words", align_bytes=64)
         nc.vector.tensor_copy(key_pairs[:], key_pool[:].bitcast(U32).indirect(offsets[:]))
-        nc.vector.tensor_copy(key_scales[:, 0, :], scale_pool[:, 0, :].indirect(offsets[:]))
         halves = key_pairs[:].bitcast(U16).rearrange("p (i o) -> p o i", o=PASSES)
-        for o in range(PASSES):
-            nc.vector.tensor_copy(key_words[:, o, :].bitcast(U16), halves[:, o, :])
 
         q_bf = sb.tile([P, PASSES, NQ, PACK], BF16, name="q_bf", align_bytes=64)
         q_codes = sb.tile([P, PASSES * NQ], U32, name="q_codes", align_bytes=64)
@@ -84,7 +76,8 @@ def tile_attend_soft_topk_kernel(tc, qT, k_words, k_scales, vT, vs, offs, out):
         for o in range(PASSES):
             nc.scalar.activation(q_bf[:, o, :, :], q_raw[:, o, :, :].rearrange("p j q -> p q j"), ACT.Copy)
         nc.vector.quantize_mx(q_codes[:].bitcast(FP8X4), q_scales[:], q_bf[:].rearrange("p o q j -> p (o q j)"))
-        nc.vector.tensor_copy(key_scales[:, 1, :], scale_pool[:, 1, :].indirect(offsets[:]))
+        for o in range(PASSES):
+            nc.vector.tensor_copy(key_words[:, o, :].bitcast(U16), halves[:, o, :])
 
         scores = ps.tile([P, N], F32, name="scores")
         for o in range(PASSES):
@@ -98,39 +91,43 @@ def tile_attend_soft_topk_kernel(tc, qT, k_words, k_scales, vT, vs, offs, out):
                 stop=(o == PASSES - 1),
             )
 
-        vs_listed = sb.tile([P, N], F32, name="vs_listed", align_bytes=64)
+        vs_listed = sb.tile([P, N], F32, name="vs_listed", tag="p_slot", align_bytes=64)
+        vs_planes = sb.tile([P, PACK, P], F32, name="vs_planes", align_bytes=64)
         vs_turned = ps.tile([P, PACK, P], F32, name="vs_turned")
-        vs_slot = sb.tile([P, PACK], F32, name="vs_slot")
         nc.vector.tensor_copy(vs_listed[:], vs_pool[:].indirect(offsets[:]))
+        nc.scalar.activation(vs_planes[:], vs_listed[:].rearrange("p (s t) -> p t s", t=PACK), ACT.Copy)
         for t in range(PACK):
-            nc.tensor.transpose(vs_turned[:, t, :], vs_listed[:, t::PACK], identity[:])
-        nc.scalar.activation(vs_slot[:], vs_turned[:, :, VS_ROW], ACT.Copy)
+            nc.tensor.transpose(vs_turned[:, t, :], vs_planes[:, t, :], identity[:])
 
-        neg_max = sb.tile([P, 1], F32, name="neg_max")
+        neg_max = sb.tile([P, 1], F32, name="neg_max", tag="m_slot", align_bytes=64)
         total = sb.tile([P, 1], F32, name="total")
-        inv_total = sb.tile([P, 1], F32, name="inv_total")
-        probs = sb.tile([P, PACK, P], F32, name="probs", align_bytes=64)
+        inv_total = late.tile([P, 1], F32, name="inv_total", align_bytes=64, offset=2048)
+        probs = sb.tile([P, PACK, P], F32, name="probs", tag="p_slot", align_bytes=64)
         nc.vector.tensor_reduce(neg_max[:], scores[:], AXIS.X, ALU.max, negate=True)
         nc.scalar.activation(
             probs[:], scores[:].rearrange("q (s t) -> q t s", t=PACK), ACT.Exp, bias=neg_max[:], accum_out=total[:]
         )
+        vs_slot = sb.tile([P, PACK], F32, name="vs_slot", tag="m_slot", align_bytes=64)
+        nc.scalar.activation(vs_slot[:], vs_turned[:, :, VS_ROW], ACT.Copy)
         probs_turned = ps.tile([P, PACK, NQ], F32, name="probs_turned")
         for t in range(PACK):
             nc.tensor.transpose(probs_turned[:, t, :], probs[:, t, :], identity[:])
 
-        v_codes = sb.tile([P, DV], U32, name="v_codes", align_bytes=64)
+        v_codes = late.tile([P, DV], U32, name="v_codes", align_bytes=64, offset=1024)
         v_scales = sb.tile([P, DV], U8, name="v_scales", align_bytes=64)
         v_bf = []
         for h in range(V_BLOCKS):
-            v_listed = sb.tile([P, N], F32, name=f"v_listed{h}", align_bytes=64)
-            v_turned = ps.tile([P, PACK, P], F32, name=f"v_turned{h}")
+            v_listed = sb.tile([P, 2, P, 2], BF16, name=f"v_listed{h}", align_bytes=64)
+            v_turned = ps.tile([P, 2, P], F32, name=f"v_turned{h}")
             v_bf.append(sb.tile([P, P, PACK], BF16, name=f"v_bf{h}", align_bytes=64))
-            nc.vector.tensor_copy(v_listed[:], v_pool[:, h, :].indirect(offsets[:]))
-            for t in range(PACK):
-                nc.tensor.transpose(v_turned[:, t, :], v_listed[:, t::PACK], identity[:])
-            nc.scalar.activation(v_bf[h][:], v_turned[:].rearrange("p t e -> p e t"), ACT.Copy)
+            nc.vector.tensor_copy(v_listed[:].rearrange("p u s c -> p s u c"), v_pool[:, h, :].indirect(offsets[:]))
+            for u in range(2):
+                nc.tensor.transpose(
+                    v_turned[:, u, :], v_listed[:, u, :, :].rearrange("p s c -> p (s c)").bitcast(F32), identity[:]
+                )
+            nc.scalar.copy(v_bf[h][:].bitcast(F32), v_turned[:].rearrange("p u e -> p e u"))
 
-        w_bf = sb.tile([P, NQ, PACK], BF16, name="w_bf", align_bytes=64)
+        w_bf = late.tile([P, NQ, PACK], BF16, name="w_bf", align_bytes=64, offset=0)
         w_codes = sb.tile([P, NQ], U32, name="w_codes", align_bytes=64)
         w_scales = sb.tile([P, NQ], U8, name="w_scales", align_bytes=64)
         nc.vector.tensor_tensor(
@@ -139,14 +136,17 @@ def tile_attend_soft_topk_kernel(tc, qT, k_words, k_scales, vT, vs, offs, out):
             vs_slot[:].unsqueeze(1).to_broadcast([P, NQ, PACK]),
             ALU.mult,
         )
-        nc.vector.reciprocal(inv_total[:], total[:])
+        nc.vector.quantize_mx(
+            v_codes[:, 0:P].bitcast(FP8X4), v_scales[:, 0:P], v_bf[0][:].rearrange("p e t -> p (e t)")
+        )
         nc.vector.quantize_mx(w_codes[:].bitcast(FP8X4), w_scales[:], w_bf[:].rearrange("p q t -> p (q t)"))
+        nc.vector.reciprocal(inv_total[:], total[:])
+        nc.vector.quantize_mx(
+            v_codes[:, P:DV].bitcast(FP8X4), v_scales[:, P:DV], v_bf[1][:].rearrange("p e t -> p (e t)")
+        )
 
         for h in range(V_BLOCKS):
             cols = slice(h * P, (h + 1) * P)
-            nc.vector.quantize_mx(
-                v_codes[:, cols].bitcast(FP8X4), v_scales[:, cols], v_bf[h][:].rearrange("p e t -> p (e t)")
-            )
             sums = ps.tile([P, P], F32, name=f"sums{h}")
             result = sb.tile([P, P], F32, name=f"result{h}")
             nc.tensor.matmul_mx(

@@ -34,41 +34,39 @@ def tile_attend_soft_topk_kernel(tc, qT, k_words, k_scales, vT, vs, offs, out):
 
         offsets = sb.tile([P, N // 16], U16, name="offsets")
         key_pool = sb.tile([P, T], I32, name="key_pool", align_bytes=64)
-        scale_pool = sb.tile([P, PASSES, T], U8, name="scale_pool", align_bytes=64)
-        vs_pool = sb.tile([P, T], F32, name="vs_pool", tag="m_slot", align_bytes=64)
+        scale_pool = sb.tile([P, T], U8, name="scale_pool", align_bytes=64)
+        moved_scales = sb.tile([P, N], U8, name="moved_scales", align_bytes=64)
+        vs_pool = sb.tile([P, T], F32, name="vs_pool", align_bytes=64)
         identity = sb.tile([P, P], F32, name="identity", align_bytes=64)
         warm_out = sb.tile([P, 8], F32, name="warm_out")
-
-        nc.gpsimd.memset(scale_pool[:, 0, :].bitcast(I32), 0)
-        nc.vector.memset(scale_pool[:, 1, :].bitcast(I32), 0)
-        nc.vector.memset(vs_pool[:], 0.0)
-        make_identity(nc, identity[:])
         q_raw = sb.tile([P, PASSES, PACK, NQ], F32, name="q_raw", align_bytes=64)
-        v_pool = late.tile([P, V_BLOCKS, T], F32, name="v_pool", align_bytes=64, offset=0)
+        v_pools = [
+            late.tile([P, T], F32, name=f"v_pool{h}", align_bytes=64, offset=h * 4 * T) for h in range(V_BLOCKS)
+        ]
+
+        nc.vector.memset(scale_pool[:].bitcast(I32), 0)
+        nc.vector.memset(vs_pool[:], 0.0)
+        nc.vector.memset(moved_scales[:].bitcast(I32), 0)
+        make_identity(nc, identity[:])
 
         nc.scalar.activation(warm_out[:], identity[:, 0:8], ACT.Exp)
         nc.sync.dma_start(offsets[:], offs)
         q_rows = qT[0].rearrange("(o p j) q -> o p j q", o=PASSES, j=PACK)
         nc.sync.dma_start(q_raw[:, 0, :, :], q_rows[0])
-        for quad in range(4):
-            nc.sync.dma_start(
-                scale_pool[32 * quad : 32 * quad + 4, :, :].bitcast(I32),
-                k_scales[:, 4 * quad : 4 * quad + 4, :].rearrange("o f t -> f o t").bitcast(I32),
-            )
-        nc.sync.dma_start(key_pool[:], k_words[0].rearrange("p t b -> p (t b)").bitcast(I32))
+        for r in range(4):
+            nc.sync.dma_start(scale_pool[r:P:32, :].bitcast(I32), k_scales[0, r:16:4, :].bitcast(I32))
+        nc.sync.dma_start(scale_pool[4:P:8, :].bitcast(I32), k_scales[1].bitcast(I32))
         nc.sync.dma_start(q_raw[:, 1, :, :], q_rows[1])
         nc.sync.dma_start(vs_pool[VS_ROW : VS_ROW + 1, :], vs[0:1, :])
+        nc.sync.dma_start(key_pool[:], k_words[0].rearrange("p t b -> p (t b)").bitcast(I32))
         for h in range(V_BLOCKS):
-            nc.sync.dma_start(v_pool[:, h, :], vT[h * P : (h + 1) * P, :])
+            nc.sync.dma_start(v_pools[h][:], vT[h * P : (h + 1) * P, :])
 
-        key_scales = sb.tile([P, PASSES, N], U8, name="key_scales", align_bytes=64)
-        for o in range(PASSES):
-            nc.vector.tensor_copy(key_scales[:, o, :], scale_pool[:, o, :].indirect(offsets[:]))
-
-        key_pairs = sb.tile([P, N], U32, name="key_pairs", align_bytes=64)
-        key_words = sb.tile([P, PASSES, 2 * N], U8, name="key_words", align_bytes=64)
-        nc.vector.tensor_copy(key_pairs[:], key_pool[:].bitcast(U32).indirect(offsets[:]))
-        halves = key_pairs[:].bitcast(U16).rearrange("p (i o) -> p o i", o=PASSES)
+        listed_scales = sb.tile([P, N], U8, name="listed_scales", align_bytes=64)
+        nc.vector.tensor_copy(listed_scales[:], scale_pool[:].indirect(offsets[:]))
+        for r in range(4):
+            nc.scalar.dma_start(moved_scales[r:P:32, :].bitcast(I32), listed_scales[4 + 8 * r : P : 32, :].bitcast(I32))
+        key_scales = (listed_scales, moved_scales)
 
         q_bf = sb.tile([P, PASSES, NQ, PACK], BF16, name="q_bf", align_bytes=64)
         q_codes = sb.tile([P, PASSES * NQ], U32, name="q_codes", align_bytes=64)
@@ -76,6 +74,21 @@ def tile_attend_soft_topk_kernel(tc, qT, k_words, k_scales, vT, vs, offs, out):
         for o in range(PASSES):
             nc.scalar.activation(q_bf[:, o, :, :], q_raw[:, o, :, :].rearrange("p j q -> p q j"), ACT.Copy)
         nc.vector.quantize_mx(q_codes[:].bitcast(FP8X4), q_scales[:], q_bf[:].rearrange("p o q j -> p (o q j)"))
+
+        vs_listed = sb.tile([P, N], F32, name="vs_listed", align_bytes=64)
+        vs_planes = sb.tile([P, PACK, P], F32, name="vs_planes", align_bytes=64)
+        vs_turned = ps.tile([P, PACK, P], F32, name="vs_turned")
+        vs_slot = sb.tile([P, PACK], F32, name="vs_slot")
+        nc.vector.tensor_copy(vs_listed[:], vs_pool[:].indirect(offsets[:]))
+        nc.scalar.activation(vs_planes[:].rearrange("p t s -> p s t"), vs_listed[:].rearrange("p (s t) -> p s t", t=PACK), ACT.Copy)
+        for t in range(PACK):
+            nc.tensor.transpose(vs_turned[:, t, :], vs_planes[:, t, :], identity[:])
+        nc.scalar.activation(vs_slot[:], vs_turned[:, :, VS_ROW], ACT.Copy)
+
+        key_pairs = sb.tile([P, N], U32, name="key_pairs", align_bytes=64)
+        key_words = sb.tile([P, PASSES, 2 * N], U8, name="key_words", align_bytes=64)
+        nc.vector.tensor_copy(key_pairs[:], key_pool[:].bitcast(U32).indirect(offsets[:]))
+        halves = key_pairs[:].bitcast(U16).rearrange("p (i o) -> p o i", o=PASSES)
         for o in range(PASSES):
             nc.vector.tensor_copy(key_words[:, o, :].bitcast(U16), halves[:, o, :])
 
@@ -86,48 +99,46 @@ def tile_attend_soft_topk_kernel(tc, qT, k_words, k_scales, vT, vs, offs, out):
                 lhsT=q_codes[:, o * NQ : (o + 1) * NQ].bitcast(FP8X4),
                 lhsT_scale=q_scales[:, o * NQ : (o + 1) * NQ],
                 rhs=key_words[:, o, :].bitcast(FP4X4),
-                rhs_scale=key_scales[:, o, :],
+                rhs_scale=key_scales[o][:],
                 start=(o == 0),
                 stop=(o == PASSES - 1),
             )
 
-        vs_listed = sb.tile([P, N], F32, name="vs_listed", tag="p_slot", align_bytes=64)
-        vs_planes = sb.tile([P, PACK, P], F32, name="vs_planes", align_bytes=64)
-        vs_turned = ps.tile([P, PACK, P], F32, name="vs_turned")
-        nc.vector.tensor_copy(vs_listed[:], vs_pool[:].indirect(offsets[:]))
-        nc.scalar.activation(vs_planes[:], vs_listed[:].rearrange("p (s t) -> p t s", t=PACK), ACT.Copy)
-        for t in range(PACK):
-            nc.tensor.transpose(vs_turned[:, t, :], vs_planes[:, t, :], identity[:])
+        v_listed = [sb.tile([P, 2, P, 2], BF16, name=f"v_listed{h}", align_bytes=64) for h in range(V_BLOCKS)]
+        nc.vector.tensor_copy(v_listed[0][:].rearrange("p u s c -> p s u c"), v_pools[0][:].indirect(offsets[:]))
 
-        neg_max = sb.tile([P, 1], F32, name="neg_max", tag="m_slot", align_bytes=64)
+        neg_max = late.tile([P, 1], F32, name="neg_max", align_bytes=64, offset=0)
         total = sb.tile([P, 1], F32, name="total")
-        inv_total = late.tile([P, 1], F32, name="inv_total", align_bytes=64, offset=2048)
-        probs = sb.tile([P, PACK, P], F32, name="probs", tag="p_slot", align_bytes=64)
+        probs = sb.tile([P, PACK, P], F32, name="probs", align_bytes=64)
         nc.vector.tensor_reduce(neg_max[:], scores[:], AXIS.X, ALU.max, negate=True)
+        nc.vector.tensor_copy(v_listed[1][:].rearrange("p u s c -> p s u c"), v_pools[1][:].indirect(offsets[:]))
         nc.scalar.activation(
             probs[:], scores[:].rearrange("q (s t) -> q t s", t=PACK), ACT.Exp, bias=neg_max[:], accum_out=total[:]
         )
-        vs_slot = sb.tile([P, PACK], F32, name="vs_slot", tag="m_slot", align_bytes=64)
-        nc.scalar.activation(vs_slot[:], vs_turned[:, :, VS_ROW], ACT.Copy)
-        probs_turned = ps.tile([P, PACK, NQ], F32, name="probs_turned")
-        for t in range(PACK):
-            nc.tensor.transpose(probs_turned[:, t, :], probs[:, t, :], identity[:])
 
-        v_codes = late.tile([P, DV], U32, name="v_codes", align_bytes=64, offset=1024)
+        v_codes = late.tile([P, DV], U32, name="v_codes", align_bytes=64, offset=4 * T + 1024)
+        inv_total = late.tile([P, 1], F32, name="inv_total", align_bytes=64, offset=4 * T + 2048)
         v_scales = sb.tile([P, DV], U8, name="v_scales", align_bytes=64)
-        v_bf = []
-        for h in range(V_BLOCKS):
-            v_listed = sb.tile([P, 2, P, 2], BF16, name=f"v_listed{h}", align_bytes=64)
+        v_bf = [
+            late.tile([P, P, PACK], BF16, name="v_bf0", align_bytes=64, offset=0),
+            sb.tile([P, P, PACK], BF16, name="v_bf1", align_bytes=64),
+        ]
+        probs_turned = ps.tile([P, PACK, NQ], F32, name="probs_turned")
+
+        def turn_values(h):
             v_turned = ps.tile([P, 2, P], F32, name=f"v_turned{h}")
-            v_bf.append(sb.tile([P, P, PACK], BF16, name=f"v_bf{h}", align_bytes=64))
-            nc.vector.tensor_copy(v_listed[:].rearrange("p u s c -> p s u c"), v_pool[:, h, :].indirect(offsets[:]))
             for u in range(2):
                 nc.tensor.transpose(
-                    v_turned[:, u, :], v_listed[:, u, :, :].rearrange("p s c -> p (s c)").bitcast(F32), identity[:]
+                    v_turned[:, u, :], v_listed[h][:, u, :, :].rearrange("p s c -> p (s c)").bitcast(F32), identity[:]
                 )
             nc.scalar.copy(v_bf[h][:].bitcast(F32), v_turned[:].rearrange("p u e -> p e u"))
 
-        w_bf = late.tile([P, NQ, PACK], BF16, name="w_bf", align_bytes=64, offset=0)
+        turn_values(0)
+        for t in range(PACK):
+            nc.tensor.transpose(probs_turned[:, t, :], probs[:, t, :], identity[:])
+        turn_values(1)
+
+        w_bf = late.tile([P, NQ, PACK], BF16, name="w_bf", align_bytes=64, offset=4 * T)
         w_codes = sb.tile([P, NQ], U32, name="w_codes", align_bytes=64)
         w_scales = sb.tile([P, NQ], U8, name="w_scales", align_bytes=64)
         nc.vector.tensor_tensor(
@@ -158,5 +169,8 @@ def tile_attend_soft_topk_kernel(tc, qT, k_words, k_scales, vT, vs, offs, out):
                 start=True,
                 stop=True,
             )
-            nc.scalar.activation(result[:], sums[:], ACT.Copy, scale=inv_total[:])
+            if h == 0:
+                nc.vector.tensor_scalar(result[:], sums[:], inv_total[:], None, ALU.mult)
+            else:
+                nc.scalar.activation(result[:], sums[:], ACT.Copy, scale=inv_total[:])
             nc.sync.dma_start(out[0][:, cols], result[:])

@@ -45,27 +45,28 @@ def tile_attend_soft_topk_kernel(tc, qT, k_words, k_scales, vT, vs, offs, out):
         ]
 
         nc.vector.memset(scale_pool[:].bitcast(I32), 0)
-        nc.vector.memset(vs_pool[:], 0.0)
+        nc.vector.memset(vs_pool[:].bitcast(I32), 0)
         nc.vector.memset(moved_scales[:].bitcast(I32), 0)
         make_identity(nc, identity[:])
 
         nc.scalar.activation(warm_out[:], identity[:, 0:8], ACT.Exp)
-        nc.sync.dma_start(offsets[:], offs)
         q_rows = qT[0].rearrange("(o p j) q -> o p j q", o=PASSES, j=PACK)
         nc.sync.dma_start(q_raw[:, 0, :, :], q_rows[0])
+        nc.sync.dma_start(offsets[:], offs)
         for r in range(4):
             nc.sync.dma_start(scale_pool[r:P:32, :].bitcast(I32), k_scales[0, r:16:4, :].bitcast(I32))
         nc.sync.dma_start(scale_pool[4:P:8, :].bitcast(I32), k_scales[1].bitcast(I32))
         nc.sync.dma_start(q_raw[:, 1, :, :], q_rows[1])
         nc.sync.dma_start(vs_pool[VS_ROW : VS_ROW + 1, :], vs[0:1, :])
         nc.sync.dma_start(key_pool[:], k_words[0].rearrange("p t b -> p (t b)").bitcast(I32))
-        for h in range(V_BLOCKS):
-            nc.sync.dma_start(v_pools[h][:], vT[h * P : (h + 1) * P, :])
+        nc.sync.dma_start(v_pools[0][:, 0 : T // 2], vT[0:P, 0 : T // 2])
 
         listed_scales = sb.tile([P, N], U8, name="listed_scales", align_bytes=64)
         nc.vector.tensor_copy(listed_scales[:], scale_pool[:].indirect(offsets[:]))
         for r in range(4):
-            nc.scalar.dma_start(moved_scales[r:P:32, :].bitcast(I32), listed_scales[4 + 8 * r : P : 32, :].bitcast(I32))
+            nc.sync.dma_start(moved_scales[r:P:32, :].bitcast(I32), listed_scales[4 + 8 * r : P : 32, :].bitcast(I32))
+        nc.sync.dma_start(v_pools[0][:, T // 2 : T], vT[0:P, T // 2 : T])
+        nc.sync.dma_start(v_pools[1][:], vT[P:DV, :])
         key_scales = (listed_scales, moved_scales)
 
         q_bf = sb.tile([P, PASSES, NQ, PACK], BF16, name="q_bf", align_bytes=64)
@@ -108,13 +109,21 @@ def tile_attend_soft_topk_kernel(tc, qT, k_words, k_scales, vT, vs, offs, out):
         nc.vector.tensor_copy(v_listed[0][:].rearrange("p u s c -> p s u c"), v_pools[0][:].indirect(offsets[:]))
 
         neg_max = late.tile([P, 1], F32, name="neg_max", align_bytes=64, offset=0)
+        half_total = sb.tile([P, 2], F32, name="half_total")
         total = sb.tile([P, 1], F32, name="total")
         probs = sb.tile([P, PACK, P], F32, name="probs", align_bytes=64)
         nc.vector.tensor_reduce(neg_max[:], scores[:], AXIS.X, ALU.max, negate=True)
         nc.vector.tensor_copy(v_listed[1][:].rearrange("p u s c -> p s u c"), v_pools[1][:].indirect(offsets[:]))
-        nc.scalar.activation(
-            probs[:], scores[:].rearrange("q (s t) -> q t s", t=PACK), ACT.Exp, bias=neg_max[:], accum_out=total[:]
-        )
+        score_planes = scores[:].rearrange("q (s t) -> q t s", t=PACK)
+        for half in range(2):
+            planes = slice(2 * half, 2 * half + 2)
+            nc.scalar.activation(
+                probs[:, planes, :],
+                score_planes[:, planes, :],
+                ACT.Exp,
+                bias=neg_max[:],
+                accum_out=half_total[:, half : half + 1],
+            )
 
         v_codes = late.tile([P, DV], U32, name="v_codes", align_bytes=64, offset=4 * T + 1024)
         inv_total = late.tile([P, 1], F32, name="inv_total", align_bytes=64, offset=4 * T + 2048)
@@ -136,6 +145,7 @@ def tile_attend_soft_topk_kernel(tc, qT, k_words, k_scales, vT, vs, offs, out):
         turn_values(0)
         for t in range(PACK):
             nc.tensor.transpose(probs_turned[:, t, :], probs[:, t, :], identity[:])
+        nc.scalar.activation(total[:], half_total[:, 0:1], ACT.Identity, bias=half_total[:, 1:2])
         turn_values(1)
 
         w_bf = late.tile([P, NQ, PACK], BF16, name="w_bf", align_bytes=64, offset=4 * T)
@@ -151,10 +161,10 @@ def tile_attend_soft_topk_kernel(tc, qT, k_words, k_scales, vT, vs, offs, out):
             v_codes[:, 0:P].bitcast(FP8X4), v_scales[:, 0:P], v_bf[0][:].rearrange("p e t -> p (e t)")
         )
         nc.vector.quantize_mx(w_codes[:].bitcast(FP8X4), w_scales[:], w_bf[:].rearrange("p q t -> p (q t)"))
-        nc.vector.reciprocal(inv_total[:], total[:])
         nc.vector.quantize_mx(
             v_codes[:, P:DV].bitcast(FP8X4), v_scales[:, P:DV], v_bf[1][:].rearrange("p e t -> p (e t)")
         )
+        nc.vector.reciprocal(inv_total[:], total[:])
 
         for h in range(V_BLOCKS):
             cols = slice(h * P, (h + 1) * P)

@@ -34,14 +34,17 @@ def tile_attend_soft_topk_kernel(tc, qT, k_words, k_scales, vT, vs, offs, out):
 
         offsets = sb.tile([P, N // 16], U16, name="offsets")
         key_pool = sb.tile([P, T], I32, name="key_pool", align_bytes=64)
-        scale_pool = sb.tile([P, T], U8, name="scale_pool", align_bytes=64)
         moved_scales = sb.tile([P, N], U8, name="moved_scales", align_bytes=64)
-        vs_pool = sb.tile([P, T], F32, name="vs_pool", align_bytes=64)
         identity = sb.tile([P, P], F32, name="identity", align_bytes=64)
-        warm_out = sb.tile([P, 8], F32, name="warm_out")
-        q_raw = sb.tile([P, PASSES, PACK, NQ], F32, name="q_raw", align_bytes=64)
+        scale_pool = late.tile([P, T], U8, name="scale_pool", align_bytes=64, offset=0)
+        vs_pool = late.tile([P, T], F32, name="vs_pool", align_bytes=64, offset=2048)
+        q_raw = [
+            sb.tile([P, PACK, NQ], F32, name="q_raw0", align_bytes=64),
+            late.tile([P, PACK, NQ], F32, name="q_raw1", align_bytes=64, offset=10240),
+        ]
+        V0_AT, V1_AT = 12288, 20480
         v_pools = [
-            late.tile([P, T], F32, name=f"v_pool{h}", align_bytes=64, offset=h * 4 * T) for h in range(V_BLOCKS)
+            late.tile([P, T], F32, name=f"v_pool{h}", align_bytes=64, offset=at) for h, at in enumerate((V0_AT, V1_AT))
         ]
 
         nc.vector.memset(scale_pool[:].bitcast(I32), 0)
@@ -49,71 +52,79 @@ def tile_attend_soft_topk_kernel(tc, qT, k_words, k_scales, vT, vs, offs, out):
         nc.vector.memset(moved_scales[:].bitcast(I32), 0)
         make_identity(nc, identity[:])
 
-        nc.scalar.activation(warm_out[:], identity[:, 0:8], ACT.Exp)
         q_rows = qT[0].rearrange("(o p j) q -> o p j q", o=PASSES, j=PACK)
-        nc.sync.dma_start(q_raw[:, 0, :, :], q_rows[0])
+        nc.sync.dma_start(q_raw[0][:], q_rows[0])
         nc.sync.dma_start(offsets[:], offs)
+        scale_rows = k_scales.bitcast(I32).rearrange("o (a r) t -> r a o t", r=4)
         for r in range(4):
-            nc.sync.dma_start(scale_pool[r:P:32, :].bitcast(I32), k_scales[0, r:16:4, :].bitcast(I32))
-        nc.sync.dma_start(scale_pool[4:P:8, :].bitcast(I32), k_scales[1].bitcast(I32))
-        nc.sync.dma_start(q_raw[:, 1, :, :], q_rows[1])
-        nc.sync.dma_start(vs_pool[VS_ROW : VS_ROW + 1, :], vs[0:1, :])
+            nc.sync.dma_start(scale_pool[r:P:16, :].bitcast(I32), scale_rows[r])
         nc.sync.dma_start(key_pool[:], k_words[0].rearrange("p t b -> p (t b)").bitcast(I32))
+        nc.sync.dma_start(vs_pool[VS_ROW : VS_ROW + 1, :], vs[0:1, :])
+        nc.sync.dma_start(q_raw[1][:], q_rows[1])
         nc.sync.dma_start(v_pools[0][:, 0 : T // 2], vT[0:P, 0 : T // 2])
 
         listed_scales = sb.tile([P, N], U8, name="listed_scales", align_bytes=64)
         nc.vector.tensor_copy(listed_scales[:], scale_pool[:].indirect(offsets[:]))
-        for r in range(4):
-            nc.sync.dma_start(moved_scales[r:P:32, :].bitcast(I32), listed_scales[4 + 8 * r : P : 32, :].bitcast(I32))
+        nc.sync.dma_start(moved_scales[0 : P - 16, :].bitcast(I32), listed_scales[16:P, :].bitcast(I32))
         nc.sync.dma_start(v_pools[0][:, T // 2 : T], vT[0:P, T // 2 : T])
         nc.sync.dma_start(v_pools[1][:], vT[P:DV, :])
         key_scales = (listed_scales, moved_scales)
 
-        q_bf = sb.tile([P, PASSES, NQ, PACK], BF16, name="q_bf", align_bytes=64)
-        q_codes = sb.tile([P, PASSES * NQ], U32, name="q_codes", align_bytes=64)
-        q_scales = sb.tile([P, PASSES * NQ], U8, name="q_scales", align_bytes=64)
+        q_bf = [
+            sb.tile([P, NQ, PACK], BF16, name="q_bf0", align_bytes=64),
+            late.tile([P, NQ, PACK], BF16, name="q_bf1", align_bytes=64, offset=28672),
+        ]
+        q_codes = [
+            late.tile([P, NQ], U32, name="q_codes0", align_bytes=64, offset=0),
+            sb.tile([P, NQ], U32, name="q_codes1", align_bytes=64),
+        ]
+        q_scales = [sb.tile([P, NQ], U8, name=f"q_scales{o}", align_bytes=64) for o in range(PASSES)]
         for o in range(PASSES):
-            nc.scalar.activation(q_bf[:, o, :, :], q_raw[:, o, :, :].rearrange("p j q -> p q j"), ACT.Copy)
-        nc.vector.quantize_mx(q_codes[:].bitcast(FP8X4), q_scales[:], q_bf[:].rearrange("p o q j -> p (o q j)"))
+            nc.scalar.activation(q_bf[o][:], q_raw[o][:].rearrange("p j q -> p q j"), ACT.Copy)
 
-        vs_listed = sb.tile([P, N], F32, name="vs_listed", align_bytes=64)
-        vs_planes = sb.tile([P, PACK, P], F32, name="vs_planes", align_bytes=64)
-        vs_turned = ps.tile([P, PACK, P], F32, name="vs_turned")
-        vs_slot = sb.tile([P, PACK], F32, name="vs_slot")
-        nc.vector.tensor_copy(vs_listed[:], vs_pool[:].indirect(offsets[:]))
-        nc.scalar.activation(vs_planes[:].rearrange("p t s -> p s t"), vs_listed[:].rearrange("p (s t) -> p s t", t=PACK), ACT.Copy)
-        for t in range(PACK):
-            nc.tensor.transpose(vs_turned[:, t, :], vs_planes[:, t, :], identity[:])
-        nc.scalar.activation(vs_slot[:], vs_turned[:, :, VS_ROW], ACT.Copy)
+        def quantise_queries(o):
+            nc.vector.quantize_mx(q_codes[o][:].bitcast(FP8X4), q_scales[o][:], q_bf[o][:].rearrange("p q j -> p (q j)"))
 
+        quantise_queries(0)
         key_pairs = sb.tile([P, N], U32, name="key_pairs", align_bytes=64)
         key_words = sb.tile([P, PASSES, 2 * N], U8, name="key_words", align_bytes=64)
         nc.vector.tensor_copy(key_pairs[:], key_pool[:].bitcast(U32).indirect(offsets[:]))
         halves = key_pairs[:].bitcast(U16).rearrange("p (i o) -> p o i", o=PASSES)
         for o in range(PASSES):
             nc.vector.tensor_copy(key_words[:, o, :].bitcast(U16), halves[:, o, :])
+        quantise_queries(1)
+
+        vs_listed = late.tile([P, N], F32, name="vs_listed", align_bytes=64, offset=28672)
+        nc.vector.tensor_copy(vs_listed[:], vs_pool[:].indirect(offsets[:]))
 
         scores = ps.tile([P, N], F32, name="scores")
         for o in range(PASSES):
             nc.tensor.matmul_mx(
                 scores[:],
-                lhsT=q_codes[:, o * NQ : (o + 1) * NQ].bitcast(FP8X4),
-                lhsT_scale=q_scales[:, o * NQ : (o + 1) * NQ],
+                lhsT=q_codes[o][:].bitcast(FP8X4),
+                lhsT_scale=q_scales[o][:],
                 rhs=key_words[:, o, :].bitcast(FP4X4),
                 rhs_scale=key_scales[o][:],
                 start=(o == 0),
                 stop=(o == PASSES - 1),
             )
 
-        v_listed = [sb.tile([P, 2, P, 2], BF16, name=f"v_listed{h}", align_bytes=64) for h in range(V_BLOCKS)]
-        nc.vector.tensor_copy(v_listed[0][:].rearrange("p u s c -> p s u c"), v_pools[0][:].indirect(offsets[:]))
+        vs_planes = late.tile([P, PACK, P], F32, name="vs_planes", align_bytes=64, offset=10240)
+        vs_turned = ps.tile([P, PACK, P], F32, name="vs_turned")
+        vs_slot = sb.tile([P, PACK], F32, name="vs_slot")
+        nc.scalar.activation(vs_planes[:].rearrange("p t s -> p s t"), vs_listed[:].rearrange("p (s t) -> p s t", t=PACK), ACT.Copy)
+        for t in range(PACK):
+            nc.tensor.transpose(vs_turned[:, t, :], vs_planes[:, t, :], identity[:])
+        nc.scalar.activation(vs_slot[:], vs_turned[:, :, VS_ROW], ACT.Copy)
 
-        neg_max = late.tile([P, 1], F32, name="neg_max", align_bytes=64, offset=0)
+        neg_max = sb.tile([P, 1], F32, name="neg_max")
         half_total = sb.tile([P, 2], F32, name="half_total")
         total = sb.tile([P, 1], F32, name="total")
         probs = sb.tile([P, PACK, P], F32, name="probs", align_bytes=64)
         nc.vector.tensor_reduce(neg_max[:], scores[:], AXIS.X, ALU.max, negate=True)
-        nc.vector.tensor_copy(v_listed[1][:].rearrange("p u s c -> p s u c"), v_pools[1][:].indirect(offsets[:]))
+        v_listed = [sb.tile([P, N], BF16, name=f"v_listed{h}", align_bytes=64) for h in range(V_BLOCKS)]
+        for h in range(V_BLOCKS):
+            nc.vector.tensor_copy(v_listed[h][:], v_pools[h][:].indirect(offsets[:]))
         score_planes = scores[:].rearrange("q (s t) -> q t s", t=PACK)
         for half in range(2):
             planes = slice(2 * half, 2 * half + 2)
@@ -125,30 +136,26 @@ def tile_attend_soft_topk_kernel(tc, qT, k_words, k_scales, vT, vs, offs, out):
                 accum_out=half_total[:, half : half + 1],
             )
 
-        v_codes = late.tile([P, DV], U32, name="v_codes", align_bytes=64, offset=4 * T + 1024)
-        inv_total = late.tile([P, 1], F32, name="inv_total", align_bytes=64, offset=4 * T + 2048)
+        v_codes = late.tile([P, DV], U32, name="v_codes", align_bytes=64, offset=V1_AT + 1024)
+        inv_total = late.tile([P, 1], F32, name="inv_total", align_bytes=64, offset=V1_AT + 2048)
         v_scales = sb.tile([P, DV], U8, name="v_scales", align_bytes=64)
-        v_bf = [
-            late.tile([P, P, PACK], BF16, name="v_bf0", align_bytes=64, offset=0),
-            sb.tile([P, P, PACK], BF16, name="v_bf1", align_bytes=64),
-        ]
+        v_bf = [sb.tile([P, P, PACK], BF16, name=f"v_bf{h}", align_bytes=64) for h in range(V_BLOCKS)]
         probs_turned = ps.tile([P, PACK, NQ], F32, name="probs_turned")
 
         def turn_values(h):
             v_turned = ps.tile([P, 2, P], F32, name=f"v_turned{h}")
+            words = v_listed[h][:].bitcast(F32)
             for u in range(2):
-                nc.tensor.transpose(
-                    v_turned[:, u, :], v_listed[h][:, u, :, :].rearrange("p s c -> p (s c)").bitcast(F32), identity[:]
-                )
+                nc.tensor.transpose(v_turned[:, u, :], words[:, u : 2 * P : 2], identity[:])
             nc.scalar.copy(v_bf[h][:].bitcast(F32), v_turned[:].rearrange("p u e -> p e u"))
 
-        turn_values(0)
         for t in range(PACK):
             nc.tensor.transpose(probs_turned[:, t, :], probs[:, t, :], identity[:])
         nc.scalar.activation(total[:], half_total[:, 0:1], ACT.Identity, bias=half_total[:, 1:2])
+        turn_values(0)
         turn_values(1)
 
-        w_bf = late.tile([P, NQ, PACK], BF16, name="w_bf", align_bytes=64, offset=4 * T)
+        w_bf = late.tile([P, NQ, PACK], BF16, name="w_bf", align_bytes=64, offset=V1_AT)
         w_codes = sb.tile([P, NQ], U32, name="w_codes", align_bytes=64)
         w_scales = sb.tile([P, NQ], U8, name="w_scales", align_bytes=64)
         nc.vector.tensor_tensor(
@@ -179,7 +186,7 @@ def tile_attend_soft_topk_kernel(tc, qT, k_words, k_scales, vT, vs, offs, out):
                 start=True,
                 stop=True,
             )
-            if h == 0:
+            if h == 1:
                 nc.vector.tensor_scalar(result[:], sums[:], inv_total[:], None, ALU.mult)
             else:
                 nc.scalar.activation(result[:], sums[:], ACT.Copy, scale=inv_total[:])

@@ -59,43 +59,41 @@ def tile_attend_soft_topk_kernel(tc, qT, k_words, k_scales, vT, vs, offs, out):
         for r in range(4):
             nc.sync.dma_start(scale_pool[r:P:16, :].bitcast(I32), scale_rows[r])
         nc.sync.dma_start(key_pool[:], k_words[0].rearrange("p t b -> p (t b)").bitcast(I32))
-        nc.sync.dma_start(vs_pool[VS_ROW : VS_ROW + 1, :], vs[0:1, :])
+        nc.scalar.dma_start(vs_pool[VS_ROW : VS_ROW + 1, :], vs[0:1, :])
         nc.sync.dma_start(q_raw[1][:], q_rows[1])
-        nc.sync.dma_start(v_pools[0][:, 0 : T // 2], vT[0:P, 0 : T // 2])
+        for h in range(V_BLOCKS):
+            nc.sync.dma_start(v_pools[h][:], vT[h * P : (h + 1) * P, :])
 
         listed_scales = sb.tile([P, N], U8, name="listed_scales", align_bytes=64)
         nc.vector.tensor_copy(listed_scales[:], scale_pool[:].indirect(offsets[:]))
-        nc.sync.dma_start(moved_scales[0 : P - 16, :].bitcast(I32), listed_scales[16:P, :].bitcast(I32))
-        nc.sync.dma_start(v_pools[0][:, T // 2 : T], vT[0:P, T // 2 : T])
-        nc.sync.dma_start(v_pools[1][:], vT[P:DV, :])
+        nc.scalar.dma_start(moved_scales[0 : P - 16, :].bitcast(I32), listed_scales[16:P, :].bitcast(I32))
         key_scales = (listed_scales, moved_scales)
 
         q_bf = [
             sb.tile([P, NQ, PACK], BF16, name="q_bf0", align_bytes=64),
-            late.tile([P, NQ, PACK], BF16, name="q_bf1", align_bytes=64, offset=28672),
+            sb.tile([P, NQ, PACK], BF16, name="q_bf1", align_bytes=64),
         ]
         q_codes = [
-            late.tile([P, NQ], U32, name="q_codes0", align_bytes=64, offset=0),
+            sb.tile([P, NQ], U32, name="q_codes0", align_bytes=64),
             sb.tile([P, NQ], U32, name="q_codes1", align_bytes=64),
         ]
         q_scales = [sb.tile([P, NQ], U8, name=f"q_scales{o}", align_bytes=64) for o in range(PASSES)]
-        for o in range(PASSES):
-            nc.scalar.activation(q_bf[o][:], q_raw[o][:].rearrange("p j q -> p q j"), ACT.Copy)
+        nc.vector.tensor_copy(q_bf[0][:], q_raw[0][:].rearrange("p j q -> p q j"))
+        nc.scalar.activation(q_bf[1][:], q_raw[1][:].rearrange("p j q -> p q j"), ACT.Copy)
 
         def quantise_queries(o):
             nc.vector.quantize_mx(q_codes[o][:].bitcast(FP8X4), q_scales[o][:], q_bf[o][:].rearrange("p q j -> p (q j)"))
 
         quantise_queries(0)
-        key_pairs = sb.tile([P, N], U32, name="key_pairs", align_bytes=64)
+        vs_listed = late.tile([P, N], F32, name="vs_listed", align_bytes=64, offset=0)
+        nc.vector.tensor_copy(vs_listed[:], vs_pool[:].indirect(offsets[:]))
+        key_pairs = late.tile([P, N], U32, name="key_pairs", align_bytes=64, offset=2048)
         key_words = sb.tile([P, PASSES, 2 * N], U8, name="key_words", align_bytes=64)
         nc.vector.tensor_copy(key_pairs[:], key_pool[:].bitcast(U32).indirect(offsets[:]))
         halves = key_pairs[:].bitcast(U16).rearrange("p (i o) -> p o i", o=PASSES)
         for o in range(PASSES):
             nc.vector.tensor_copy(key_words[:, o, :].bitcast(U16), halves[:, o, :])
         quantise_queries(1)
-
-        vs_listed = late.tile([P, N], F32, name="vs_listed", align_bytes=64, offset=28672)
-        nc.vector.tensor_copy(vs_listed[:], vs_pool[:].indirect(offsets[:]))
 
         scores = ps.tile([P, N], F32, name="scores")
         for o in range(PASSES):
@@ -117,14 +115,14 @@ def tile_attend_soft_topk_kernel(tc, qT, k_words, k_scales, vT, vs, offs, out):
             nc.tensor.transpose(vs_turned[:, t, :], vs_planes[:, t, :], identity[:])
         nc.scalar.activation(vs_slot[:], vs_turned[:, :, VS_ROW], ACT.Copy)
 
-        neg_max = sb.tile([P, 1], F32, name="neg_max")
+        neg_max = late.tile([P, 1], F32, name="neg_max", align_bytes=64, offset=V0_AT)
         half_total = sb.tile([P, 2], F32, name="half_total")
         total = sb.tile([P, 1], F32, name="total")
         probs = sb.tile([P, PACK, P], F32, name="probs", align_bytes=64)
-        nc.vector.tensor_reduce(neg_max[:], scores[:], AXIS.X, ALU.max, negate=True)
         v_listed = [sb.tile([P, N], BF16, name=f"v_listed{h}", align_bytes=64) for h in range(V_BLOCKS)]
-        for h in range(V_BLOCKS):
-            nc.vector.tensor_copy(v_listed[h][:], v_pools[h][:].indirect(offsets[:]))
+        nc.vector.tensor_copy(v_listed[0][:], v_pools[0][:].indirect(offsets[:]))
+        nc.vector.tensor_reduce(neg_max[:], scores[:], AXIS.X, ALU.max, negate=True)
+        nc.vector.tensor_copy(v_listed[1][:], v_pools[1][:].indirect(offsets[:]))
         score_planes = scores[:].rearrange("q (s t) -> q t s", t=PACK)
         for half in range(2):
             planes = slice(2 * half, 2 * half + 2)
@@ -136,9 +134,9 @@ def tile_attend_soft_topk_kernel(tc, qT, k_words, k_scales, vT, vs, offs, out):
                 accum_out=half_total[:, half : half + 1],
             )
 
-        v_codes = late.tile([P, DV], U32, name="v_codes", align_bytes=64, offset=V1_AT + 1024)
+        v_codes = [sb.tile([P, P], U32, name=f"v_codes{h}", align_bytes=64) for h in range(V_BLOCKS)]
         inv_total = late.tile([P, 1], F32, name="inv_total", align_bytes=64, offset=V1_AT + 2048)
-        v_scales = sb.tile([P, DV], U8, name="v_scales", align_bytes=64)
+        v_scales = [sb.tile([P, P], U8, name=f"v_scales{h}", align_bytes=64) for h in range(V_BLOCKS)]
         v_bf = [sb.tile([P, P, PACK], BF16, name=f"v_bf{h}", align_bytes=64) for h in range(V_BLOCKS)]
         probs_turned = ps.tile([P, PACK, NQ], F32, name="probs_turned")
 
@@ -149,10 +147,14 @@ def tile_attend_soft_topk_kernel(tc, qT, k_words, k_scales, vT, vs, offs, out):
                 nc.tensor.transpose(v_turned[:, u, :], words[:, u : 2 * P : 2], identity[:])
             nc.scalar.copy(v_bf[h][:].bitcast(F32), v_turned[:].rearrange("p u e -> p e u"))
 
+        def quantise_values(h):
+            nc.vector.quantize_mx(v_codes[h][:].bitcast(FP8X4), v_scales[h][:], v_bf[h][:].rearrange("p e t -> p (e t)"))
+
+        turn_values(0)
+        quantise_values(0)
         for t in range(PACK):
             nc.tensor.transpose(probs_turned[:, t, :], probs[:, t, :], identity[:])
         nc.scalar.activation(total[:], half_total[:, 0:1], ACT.Identity, bias=half_total[:, 1:2])
-        turn_values(0)
         turn_values(1)
 
         w_bf = late.tile([P, NQ, PACK], BF16, name="w_bf", align_bytes=64, offset=V1_AT)
@@ -164,14 +166,9 @@ def tile_attend_soft_topk_kernel(tc, qT, k_words, k_scales, vT, vs, offs, out):
             vs_slot[:].unsqueeze(1).to_broadcast([P, NQ, PACK]),
             ALU.mult,
         )
-        nc.vector.quantize_mx(
-            v_codes[:, 0:P].bitcast(FP8X4), v_scales[:, 0:P], v_bf[0][:].rearrange("p e t -> p (e t)")
-        )
-        nc.vector.quantize_mx(w_codes[:].bitcast(FP8X4), w_scales[:], w_bf[:].rearrange("p q t -> p (q t)"))
-        nc.vector.quantize_mx(
-            v_codes[:, P:DV].bitcast(FP8X4), v_scales[:, P:DV], v_bf[1][:].rearrange("p e t -> p (e t)")
-        )
         nc.vector.reciprocal(inv_total[:], total[:])
+        nc.vector.quantize_mx(w_codes[:].bitcast(FP8X4), w_scales[:], w_bf[:].rearrange("p q t -> p (q t)"))
+        quantise_values(1)
 
         for h in range(V_BLOCKS):
             cols = slice(h * P, (h + 1) * P)
@@ -181,8 +178,8 @@ def tile_attend_soft_topk_kernel(tc, qT, k_words, k_scales, vT, vs, offs, out):
                 sums[:],
                 lhsT=w_codes[:].bitcast(FP8X4),
                 lhsT_scale=w_scales[:],
-                rhs=v_codes[:, cols].bitcast(FP8X4),
-                rhs_scale=v_scales[:, cols],
+                rhs=v_codes[h][:].bitcast(FP8X4),
+                rhs_scale=v_scales[h][:],
                 start=True,
                 stop=True,
             )

@@ -20,7 +20,7 @@ PACK = 4
 N, T, D, DV, NQ = 512, 2048, 1024, 256, 128
 PASSES = D // (P * PACK)
 V_BLOCKS = DV // P
-VS_ROW = 8
+VS_ROW = 127
 
 FLOPS = 2 * NQ * N * (D + DV)
 
@@ -36,37 +36,41 @@ def tile_attend_soft_topk_kernel(tc, qT, k_words, k_scales, vT, vs, offs, out):
         key_pool = sb.tile([P, T], I32, name="key_pool", align_bytes=64)
         moved_scales = sb.tile([P, N], U8, name="moved_scales", align_bytes=64)
         identity = sb.tile([P, P], F32, name="identity", align_bytes=64)
-        scale_pool = late.tile([P, T], U8, name="scale_pool", align_bytes=64, offset=0)
-        vs_pool = late.tile([P, T], F32, name="vs_pool", align_bytes=64, offset=2048)
+        scale_pool = late.tile([P, T], U8, name="scale_pool", align_bytes=64, offset=10176)
+        vs_pool = late.tile([P, T], F32, name="vs_pool", align_bytes=64, offset=20480)
         q_raw = [
             sb.tile([P, PACK, NQ], F32, name="q_raw0", align_bytes=64),
-            late.tile([P, PACK, NQ], F32, name="q_raw1", align_bytes=64, offset=10240),
+            sb.tile([P, PACK, NQ], F32, name="q_raw1", align_bytes=64),
         ]
-        V0_AT, V1_AT = 12288, 20480
+        V0_AT, V1_AT = 0, 12160
         v_pools = [
             late.tile([P, T], F32, name=f"v_pool{h}", align_bytes=64, offset=at) for h, at in enumerate((V0_AT, V1_AT))
         ]
 
         nc.vector.memset(scale_pool[:].bitcast(I32), 0)
-        nc.vector.memset(vs_pool[:].bitcast(I32), 0)
+        nc.vector.memset(vs_pool[0:VS_ROW, :], 0.0)
         nc.vector.memset(moved_scales[:].bitcast(I32), 0)
         make_identity(nc, identity[:])
 
         q_rows = qT[0].rearrange("(o p j) q -> o p j q", o=PASSES, j=PACK)
-        nc.sync.dma_start(q_raw[0][:], q_rows[0])
         nc.sync.dma_start(offsets[:], offs)
+        nc.sync.dma_start(q_raw[0][:], q_rows[0])
         scale_rows = k_scales.bitcast(I32).rearrange("o (a r) t -> r a o t", r=4)
         for r in range(4):
             nc.sync.dma_start(scale_pool[r:P:16, :].bitcast(I32), scale_rows[r])
         nc.sync.dma_start(key_pool[:], k_words[0].rearrange("p t b -> p (t b)").bitcast(I32))
         nc.scalar.dma_start(vs_pool[VS_ROW : VS_ROW + 1, :], vs[0:1, :])
         nc.sync.dma_start(q_raw[1][:], q_rows[1])
-        for h in range(V_BLOCKS):
-            nc.sync.dma_start(v_pools[h][:], vT[h * P : (h + 1) * P, :])
+        nc.sync.dma_start(v_pools[0][:], vT[0:P, :])
 
-        listed_scales = sb.tile([P, N], U8, name="listed_scales", align_bytes=64)
+        vs_listed = sb.tile([P, N], F32, name="vs_listed", align_bytes=64)
+        nc.vector.tensor_copy(vs_listed[:], vs_pool[:].indirect(offsets[:]))
+
+        listed_scales = late.tile([P, N], U8, name="listed_scales", align_bytes=64, offset=20480)
         nc.vector.tensor_copy(listed_scales[:], scale_pool[:].indirect(offsets[:]))
-        nc.scalar.dma_start(moved_scales[0 : P - 16, :].bitcast(I32), listed_scales[16:P, :].bitcast(I32))
+        for r in range(4):
+            nc.sync.dma_start(moved_scales[r:P:32, :].bitcast(I32), listed_scales[16 + r : P : 32, :].bitcast(I32))
+        nc.sync.dma_start(v_pools[1][:], vT[P:DV, :])
         key_scales = (listed_scales, moved_scales)
 
         q_bf = [
@@ -74,20 +78,25 @@ def tile_attend_soft_topk_kernel(tc, qT, k_words, k_scales, vT, vs, offs, out):
             sb.tile([P, NQ, PACK], BF16, name="q_bf1", align_bytes=64),
         ]
         q_codes = [
-            sb.tile([P, NQ], U32, name="q_codes0", align_bytes=64),
+            late.tile([P, NQ], U32, name="q_codes0", align_bytes=64, offset=10240),
             sb.tile([P, NQ], U32, name="q_codes1", align_bytes=64),
         ]
         q_scales = [sb.tile([P, NQ], U8, name=f"q_scales{o}", align_bytes=64) for o in range(PASSES)]
-        nc.vector.tensor_copy(q_bf[0][:], q_raw[0][:].rearrange("p j q -> p q j"))
+        nc.scalar.activation(q_bf[0][:], q_raw[0][:].rearrange("p j q -> p q j"), ACT.Copy)
+        vs_planes = sb.tile([P, PACK, P], F32, name="vs_planes", align_bytes=64)
+        vs_turned = ps.tile([P, PACK, P], F32, name="vs_turned")
+        vs_slot = sb.tile([P, PACK], F32, name="vs_slot")
+        nc.scalar.activation(vs_planes[:].rearrange("p t s -> p s t"), vs_listed[:].rearrange("p (s t) -> p s t", t=PACK), ACT.Copy)
+        for t in range(PACK):
+            nc.tensor.transpose(vs_turned[:, t, :], vs_planes[:, t, :], identity[:])
+        nc.scalar.activation(vs_slot[:], vs_turned[:, :, VS_ROW], ACT.Copy)
         nc.scalar.activation(q_bf[1][:], q_raw[1][:].rearrange("p j q -> p q j"), ACT.Copy)
 
         def quantise_queries(o):
             nc.vector.quantize_mx(q_codes[o][:].bitcast(FP8X4), q_scales[o][:], q_bf[o][:].rearrange("p q j -> p (q j)"))
 
         quantise_queries(0)
-        vs_listed = late.tile([P, N], F32, name="vs_listed", align_bytes=64, offset=0)
-        nc.vector.tensor_copy(vs_listed[:], vs_pool[:].indirect(offsets[:]))
-        key_pairs = late.tile([P, N], U32, name="key_pairs", align_bytes=64, offset=2048)
+        key_pairs = late.tile([P, N], U32, name="key_pairs", align_bytes=64, offset=8192)
         key_words = sb.tile([P, PASSES, 2 * N], U8, name="key_words", align_bytes=64)
         nc.vector.tensor_copy(key_pairs[:], key_pool[:].bitcast(U32).indirect(offsets[:]))
         halves = key_pairs[:].bitcast(U16).rearrange("p (i o) -> p o i", o=PASSES)
@@ -106,14 +115,6 @@ def tile_attend_soft_topk_kernel(tc, qT, k_words, k_scales, vT, vs, offs, out):
                 start=(o == 0),
                 stop=(o == PASSES - 1),
             )
-
-        vs_planes = late.tile([P, PACK, P], F32, name="vs_planes", align_bytes=64, offset=10240)
-        vs_turned = ps.tile([P, PACK, P], F32, name="vs_turned")
-        vs_slot = sb.tile([P, PACK], F32, name="vs_slot")
-        nc.scalar.activation(vs_planes[:].rearrange("p t s -> p s t"), vs_listed[:].rearrange("p (s t) -> p s t", t=PACK), ACT.Copy)
-        for t in range(PACK):
-            nc.tensor.transpose(vs_turned[:, t, :], vs_planes[:, t, :], identity[:])
-        nc.scalar.activation(vs_slot[:], vs_turned[:, :, VS_ROW], ACT.Copy)
 
         neg_max = late.tile([P, 1], F32, name="neg_max", align_bytes=64, offset=V0_AT)
         half_total = sb.tile([P, 2], F32, name="half_total")
@@ -134,7 +135,7 @@ def tile_attend_soft_topk_kernel(tc, qT, k_words, k_scales, vT, vs, offs, out):
                 accum_out=half_total[:, half : half + 1],
             )
 
-        v_codes = [sb.tile([P, P], U32, name=f"v_codes{h}", align_bytes=64) for h in range(V_BLOCKS)]
+        v_codes = [late.tile([P, P], U32, name=f"v_codes{h}", align_bytes=64, offset=V1_AT + 1024 + 512 * h) for h in range(V_BLOCKS)]
         inv_total = late.tile([P, 1], F32, name="inv_total", align_bytes=64, offset=V1_AT + 2048)
         v_scales = [sb.tile([P, P], U8, name=f"v_scales{h}", align_bytes=64) for h in range(V_BLOCKS)]
         v_bf = [sb.tile([P, P, PACK], BF16, name=f"v_bf{h}", align_bytes=64) for h in range(V_BLOCKS)]
@@ -151,7 +152,6 @@ def tile_attend_soft_topk_kernel(tc, qT, k_words, k_scales, vT, vs, offs, out):
             nc.vector.quantize_mx(v_codes[h][:].bitcast(FP8X4), v_scales[h][:], v_bf[h][:].rearrange("p e t -> p (e t)"))
 
         turn_values(0)
-        quantise_values(0)
         for t in range(PACK):
             nc.tensor.transpose(probs_turned[:, t, :], probs[:, t, :], identity[:])
         nc.scalar.activation(total[:], half_total[:, 0:1], ACT.Identity, bias=half_total[:, 1:2])
@@ -166,6 +166,7 @@ def tile_attend_soft_topk_kernel(tc, qT, k_words, k_scales, vT, vs, offs, out):
             vs_slot[:].unsqueeze(1).to_broadcast([P, NQ, PACK]),
             ALU.mult,
         )
+        quantise_values(0)
         nc.vector.reciprocal(inv_total[:], total[:])
         nc.vector.quantize_mx(w_codes[:].bitcast(FP8X4), w_scales[:], w_bf[:].rearrange("p q t -> p (q t)"))
         quantise_values(1)

@@ -31,6 +31,7 @@ def tile_attend_soft_topk_kernel(tc, qT, k_words, k_scales, vT, vs, offs, out):
         sb = ctx.enter_context(tc.tile_pool(name="sb", bufs=1))
         late = ctx.enter_context(tc.tile_pool(name="late", bufs=1))
         ps = ctx.enter_context(tc.psum_pool(name="ps", bufs=1))
+        shared_bank = ctx.enter_context(tc.psum_pool(name="shared_bank", bufs=1))
 
         offsets = sb.tile([P, N // 16], U16, name="offsets")
         key_pool = sb.tile([P, T], I32, name="key_pool", align_bytes=64)
@@ -42,14 +43,16 @@ def tile_attend_soft_topk_kernel(tc, qT, k_words, k_scales, vT, vs, offs, out):
             sb.tile([P, PACK, NQ], F32, name="q_raw0", align_bytes=64),
             sb.tile([P, PACK, NQ], F32, name="q_raw1", align_bytes=64),
         ]
-        V0_AT, V1_AT = 0, 12160
+        V0_AT, V1_AT = 0, 12288
+        V_AHEAD = 5 * T // 8
         v_pools = [
             late.tile([P, T], F32, name=f"v_pool{h}", align_bytes=64, offset=at) for h, at in enumerate((V0_AT, V1_AT))
         ]
 
         nc.vector.memset(scale_pool[:].bitcast(I32), 0)
-        nc.vector.memset(vs_pool[0:VS_ROW, :], 0.0)
         nc.vector.memset(moved_scales[:].bitcast(I32), 0)
+        nc.vector.memset(vs_pool[0:VS_ROW, 0 : T // 2], 0.0)
+        nc.gpsimd.memset(vs_pool[0:VS_ROW, T // 2 : T], 0.0)
         make_identity(nc, identity[:])
 
         q_rows = qT[0].rearrange("(o p j) q -> o p j q", o=PASSES, j=PACK)
@@ -61,7 +64,7 @@ def tile_attend_soft_topk_kernel(tc, qT, k_words, k_scales, vT, vs, offs, out):
         nc.sync.dma_start(key_pool[:], k_words[0].rearrange("p t b -> p (t b)").bitcast(I32))
         nc.scalar.dma_start(vs_pool[VS_ROW : VS_ROW + 1, :], vs[0:1, :])
         nc.sync.dma_start(q_raw[1][:], q_rows[1])
-        nc.sync.dma_start(v_pools[0][:], vT[0:P, :])
+        nc.sync.dma_start(v_pools[0][:, 0:V_AHEAD], vT[0:P, 0:V_AHEAD])
 
         vs_listed = sb.tile([P, N], F32, name="vs_listed", align_bytes=64)
         nc.vector.tensor_copy(vs_listed[:], vs_pool[:].indirect(offsets[:]))
@@ -70,6 +73,7 @@ def tile_attend_soft_topk_kernel(tc, qT, k_words, k_scales, vT, vs, offs, out):
         nc.vector.tensor_copy(listed_scales[:], scale_pool[:].indirect(offsets[:]))
         for r in range(4):
             nc.sync.dma_start(moved_scales[r:P:32, :].bitcast(I32), listed_scales[16 + r : P : 32, :].bitcast(I32))
+        nc.sync.dma_start(v_pools[0][:, V_AHEAD:T], vT[0:P, V_AHEAD:T])
         nc.sync.dma_start(v_pools[1][:], vT[P:DV, :])
         key_scales = (listed_scales, moved_scales)
 
@@ -104,7 +108,7 @@ def tile_attend_soft_topk_kernel(tc, qT, k_words, k_scales, vT, vs, offs, out):
             nc.vector.tensor_copy(key_words[:, o, :].bitcast(U16), halves[:, o, :])
         quantise_queries(1)
 
-        scores = ps.tile([P, N], F32, name="scores")
+        scores = shared_bank.tile([P, N], F32, name="scores", offset=0)
         for o in range(PASSES):
             nc.tensor.matmul_mx(
                 scores[:],
@@ -142,7 +146,7 @@ def tile_attend_soft_topk_kernel(tc, qT, k_words, k_scales, vT, vs, offs, out):
         probs_turned = ps.tile([P, PACK, NQ], F32, name="probs_turned")
 
         def turn_values(h):
-            v_turned = ps.tile([P, 2, P], F32, name=f"v_turned{h}")
+            v_turned = (ps.tile([P, 2, P], F32, name="v_turned0") if h == 0 else shared_bank.tile([P, 2, P], F32, name="v_turned1", offset=0))
             words = v_listed[h][:].bitcast(F32)
             for u in range(2):
                 nc.tensor.transpose(v_turned[:, u, :], words[:, u : 2 * P : 2], identity[:])

@@ -51,18 +51,17 @@ def tile_attend_soft_topk_kernel(tc, qT, k_words, k_scales, vT, vs, offs, out):
 
         nc.vector.memset(scale_pool[:].bitcast(I32), 0)
         nc.vector.memset(moved_scales[:].bitcast(I32), 0)
-        nc.vector.memset(vs_pool[0:VS_ROW, 0 : T // 2], 0.0)
-        nc.gpsimd.memset(vs_pool[0:VS_ROW, T // 2 : T], 0.0)
+        nc.vector.memset(vs_pool[0:VS_ROW, :].bitcast(I32), 0)
         make_identity(nc, identity[:])
 
         q_rows = qT[0].rearrange("(o p j) q -> o p j q", o=PASSES, j=PACK)
         nc.sync.dma_start(offsets[:], offs)
+        nc.sync.dma_start(vs_pool[VS_ROW : VS_ROW + 1, :], vs[0:1, :])
         nc.sync.dma_start(q_raw[0][:], q_rows[0])
         scale_rows = k_scales.bitcast(I32).rearrange("o (a r) t -> r a o t", r=4)
         for r in range(4):
             nc.sync.dma_start(scale_pool[r:P:16, :].bitcast(I32), scale_rows[r])
         nc.sync.dma_start(key_pool[:], k_words[0].rearrange("p t b -> p (t b)").bitcast(I32))
-        nc.scalar.dma_start(vs_pool[VS_ROW : VS_ROW + 1, :], vs[0:1, :])
         nc.sync.dma_start(q_raw[1][:], q_rows[1])
         nc.sync.dma_start(v_pools[0][:, 0:V_AHEAD], vT[0:P, 0:V_AHEAD])
 

@@ -44,7 +44,7 @@ def tile_attend_soft_topk_kernel(tc, qT, k_words, k_scales, vT, vs, offs, out):
             sb.tile([P, PACK, NQ], F32, name="q_raw1", align_bytes=64),
         ]
         V0_AT, V1_AT = 0, 12288
-        V_AHEAD = 5 * T // 8
+        V_AHEAD = 7 * T // 8
         v_pools = [
             late.tile([P, T], F32, name=f"v_pool{h}", align_bytes=64, offset=at) for h, at in enumerate((V0_AT, V1_AT))
         ]
@@ -170,9 +170,9 @@ def tile_attend_soft_topk_kernel(tc, qT, k_words, k_scales, vT, vs, offs, out):
             ALU.mult,
         )
         quantise_values(0)
-        nc.vector.reciprocal(inv_total[:], total[:])
         nc.vector.quantize_mx(w_codes[:].bitcast(FP8X4), w_scales[:], w_bf[:].rearrange("p q t -> p (q t)"))
         quantise_values(1)
+        nc.vector.reciprocal(inv_total[:], total[:])
 
         for h in range(V_BLOCKS):
             cols = slice(h * P, (h + 1) * P)

@@ -55,9 +55,9 @@ def tile_attend_soft_topk_kernel(tc, qT, k_words, k_scales, vT, vs, offs, out):
         make_identity(nc, identity[:])
 
         q_rows = qT[0].rearrange("(o p j) q -> o p j q", o=PASSES, j=PACK)
+        nc.sync.dma_start(q_raw[0][:], q_rows[0])
         nc.sync.dma_start(offsets[:], offs)
         nc.sync.dma_start(vs_pool[VS_ROW : VS_ROW + 1, :], vs[0:1, :])
-        nc.sync.dma_start(q_raw[0][:], q_rows[0])
         scale_rows = k_scales.bitcast(I32).rearrange("o (a r) t -> r a o t", r=4)
         for r in range(4):
             nc.sync.dma_start(scale_pool[r:P:16, :].bitcast(I32), scale_rows[r])

@@ -33,78 +33,69 @@ def tile_attend_soft_topk_kernel(tc, qT, k_words, k_scales, vT, vs, offs, out):
         ps = ctx.enter_context(tc.psum_pool(name="ps", bufs=1))
         shared_bank = ctx.enter_context(tc.psum_pool(name="shared_bank", bufs=1))
 
+        V0_AT, V1_AT, Q0_AT, Q1_AT = 0, 8192, 16384, 18432
+        SCALES_FROM = 96
+
         offsets = sb.tile([P, N // 16], U16, name="offsets")
         key_pool = sb.tile([P, T], I32, name="key_pool", align_bytes=64)
-        moved_scales = sb.tile([P, N], U8, name="moved_scales", align_bytes=64)
+        key_scales = sb.tile([P, PASSES, N], U8, name="key_scales", align_bytes=64)
         identity = sb.tile([P, P], F32, name="identity", align_bytes=64)
-        scale_pool = late.tile([P, T], U8, name="scale_pool", align_bytes=64, offset=10176)
-        vs_pool = late.tile([P, T], F32, name="vs_pool", align_bytes=64, offset=20480)
-        q_raw = [
-            sb.tile([P, PACK, NQ], F32, name="q_raw0", align_bytes=64),
-            sb.tile([P, PACK, NQ], F32, name="q_raw1", align_bytes=64),
-        ]
-        V0_AT, V1_AT = 0, 12288
-        V_AHEAD = 7 * T // 8
-        v_pools = [
-            late.tile([P, T], F32, name=f"v_pool{h}", align_bytes=64, offset=at) for h, at in enumerate((V0_AT, V1_AT))
-        ]
+        scale_pool = late.tile([P, T], U8, name="scale_pool", align_bytes=64, offset=V1_AT - T // 2)
+        vs_pool = sb.tile([P, T], F32, name="vs_pool", align_bytes=64)
+        q_raw = [late.tile([P, PACK, NQ], F32, name=f"q_raw{o}", align_bytes=64, offset=at) for o, at in enumerate((Q0_AT, Q1_AT))]
+        v_pools = [late.tile([P, T], F32, name=f"v_pool{h}", align_bytes=64, offset=at) for h, at in enumerate((V0_AT, V1_AT))]
 
-        nc.vector.memset(scale_pool[:].bitcast(I32), 0)
-        nc.vector.memset(moved_scales[:].bitcast(I32), 0)
+        nc.vector.memset(scale_pool[0:SCALES_FROM, :].bitcast(I32), 0)
+        nc.vector.memset(key_scales[:].rearrange("p o i -> p (o i)").bitcast(I32), 0)
         nc.vector.memset(vs_pool[0:VS_ROW, :].bitcast(I32), 0)
         make_identity(nc, identity[:])
 
         q_rows = qT[0].rearrange("(o p j) q -> o p j q", o=PASSES, j=PACK)
-        nc.sync.dma_start(q_raw[0][:], q_rows[0])
         nc.sync.dma_start(offsets[:], offs)
+        nc.sync.dma_start(scale_pool[SCALES_FROM:P, :].bitcast(I32), k_scales.bitcast(I32).rearrange("o f t -> f o t"))
         nc.sync.dma_start(vs_pool[VS_ROW : VS_ROW + 1, :], vs[0:1, :])
-        scale_rows = k_scales.bitcast(I32).rearrange("o (a r) t -> r a o t", r=4)
-        for r in range(4):
-            nc.sync.dma_start(scale_pool[r:P:16, :].bitcast(I32), scale_rows[r])
         nc.sync.dma_start(key_pool[:], k_words[0].rearrange("p t b -> p (t b)").bitcast(I32))
-        nc.sync.dma_start(q_raw[1][:], q_rows[1])
-        nc.sync.dma_start(v_pools[0][:, 0:V_AHEAD], vT[0:P, 0:V_AHEAD])
+        for o in range(PASSES):
+            nc.sync.dma_start(q_raw[o][:], q_rows[o])
+
+        listed_scales = sb.tile([P, N], U8, name="listed_scales", align_bytes=64)
+        nc.vector.tensor_copy(listed_scales[:], scale_pool[:].indirect(offsets[:]))
+        for a in range(4):
+            rows = slice(SCALES_FROM + 8 * a, SCALES_FROM + 8 * a + 8)
+            nc.sync.dma_start(key_scales[32 * a : 32 * a + 4, :, :].bitcast(I32), listed_scales[rows, :].bitcast(I32))
+        for h in range(V_BLOCKS):
+            nc.sync.dma_start(v_pools[h][:], vT[h * P : (h + 1) * P, :])
 
         vs_listed = sb.tile([P, N], F32, name="vs_listed", align_bytes=64)
         nc.vector.tensor_copy(vs_listed[:], vs_pool[:].indirect(offsets[:]))
+        vs_turned = ps.tile([P, PACK, P], F32, name="vs_turned")
+        for t in range(PACK):
+            nc.tensor.transpose(vs_turned[:, t, :], vs_listed[:, t:N:PACK], identity[:])
 
-        listed_scales = late.tile([P, N], U8, name="listed_scales", align_bytes=64, offset=20480)
-        nc.vector.tensor_copy(listed_scales[:], scale_pool[:].indirect(offsets[:]))
-        for r in range(4):
-            nc.sync.dma_start(moved_scales[r:P:32, :].bitcast(I32), listed_scales[16 + r : P : 32, :].bitcast(I32))
-        nc.sync.dma_start(v_pools[0][:, V_AHEAD:T], vT[0:P, V_AHEAD:T])
-        nc.sync.dma_start(v_pools[1][:], vT[P:DV, :])
-        key_scales = (listed_scales, moved_scales)
-
-        q_bf = [
-            sb.tile([P, NQ, PACK], BF16, name="q_bf0", align_bytes=64),
-            sb.tile([P, NQ, PACK], BF16, name="q_bf1", align_bytes=64),
-        ]
+        q_bf = [sb.tile([P, NQ, PACK], BF16, name=f"q_bf{o}", align_bytes=64) for o in range(PASSES)]
         q_codes = [
-            late.tile([P, NQ], U32, name="q_codes0", align_bytes=64, offset=10240),
+            sb.tile([P, NQ], U32, name="q_codes0", align_bytes=64),
             sb.tile([P, NQ], U32, name="q_codes1", align_bytes=64),
         ]
         q_scales = [sb.tile([P, NQ], U8, name=f"q_scales{o}", align_bytes=64) for o in range(PASSES)]
-        nc.scalar.activation(q_bf[0][:], q_raw[0][:].rearrange("p j q -> p q j"), ACT.Copy)
-        vs_planes = sb.tile([P, PACK, P], F32, name="vs_planes", align_bytes=64)
-        vs_turned = ps.tile([P, PACK, P], F32, name="vs_turned")
-        vs_slot = sb.tile([P, PACK], F32, name="vs_slot")
-        nc.scalar.activation(vs_planes[:].rearrange("p t s -> p s t"), vs_listed[:].rearrange("p (s t) -> p s t", t=PACK), ACT.Copy)
-        for t in range(PACK):
-            nc.tensor.transpose(vs_turned[:, t, :], vs_planes[:, t, :], identity[:])
+        for o in range(PASSES):
+            nc.scalar.activation(q_bf[o][:], q_raw[o][:].rearrange("p j q -> p q j"), ACT.Copy)
+        vs_slot = late.tile([P, PACK], F32, name="vs_slot", align_bytes=64, offset=Q1_AT)
         nc.scalar.activation(vs_slot[:], vs_turned[:, :, VS_ROW], ACT.Copy)
-        nc.scalar.activation(q_bf[1][:], q_raw[1][:].rearrange("p j q -> p q j"), ACT.Copy)
 
         def quantise_queries(o):
             nc.vector.quantize_mx(q_codes[o][:].bitcast(FP8X4), q_scales[o][:], q_bf[o][:].rearrange("p q j -> p (q j)"))
 
-        quantise_queries(0)
-        key_pairs = late.tile([P, N], U32, name="key_pairs", align_bytes=64, offset=8192)
-        key_words = sb.tile([P, PASSES, 2 * N], U8, name="key_words", align_bytes=64)
+        key_pairs = sb.tile([P, N], U32, name="key_pairs", align_bytes=64)
+        key_words = [
+            late.tile([P, 2 * N], U8, name="key_words0", align_bytes=64, offset=Q0_AT),
+            late.tile([P, 2 * N], U8, name="key_words1", align_bytes=64, offset=Q1_AT + 1024),
+        ]
         nc.vector.tensor_copy(key_pairs[:], key_pool[:].bitcast(U32).indirect(offsets[:]))
         halves = key_pairs[:].bitcast(U16).rearrange("p (i o) -> p o i", o=PASSES)
+        quantise_queries(0)
         for o in range(PASSES):
-            nc.vector.tensor_copy(key_words[:, o, :].bitcast(U16), halves[:, o, :])
+            nc.vector.tensor_copy(key_words[o][:].bitcast(U16), halves[:, o, :])
         quantise_queries(1)
 
         scores = shared_bank.tile([P, N], F32, name="scores", offset=0)
@@ -113,8 +104,8 @@ def tile_attend_soft_topk_kernel(tc, qT, k_words, k_scales, vT, vs, offs, out):
                 scores[:],
                 lhsT=q_codes[o][:].bitcast(FP8X4),
                 lhsT_scale=q_scales[o][:],
-                rhs=key_words[:, o, :].bitcast(FP4X4),
-                rhs_scale=key_scales[o][:],
+                rhs=key_words[o][:].bitcast(FP4X4),
+                rhs_scale=key_scales[:, o, :],
                 start=(o == 0),
                 stop=(o == PASSES - 1),
             )
@@ -123,11 +114,15 @@ def tile_attend_soft_topk_kernel(tc, qT, k_words, k_scales, vT, vs, offs, out):
         half_total = sb.tile([P, 2], F32, name="half_total")
         total = sb.tile([P, 1], F32, name="total")
         probs = sb.tile([P, PACK, P], F32, name="probs", align_bytes=64)
-        v_listed = [sb.tile([P, N], BF16, name=f"v_listed{h}", align_bytes=64) for h in range(V_BLOCKS)]
+        v_listed = [
+            sb.tile([P, N], BF16, name="v_listed0", align_bytes=64),
+            sb.tile([P, N], BF16, name="v_listed1", align_bytes=64),
+        ]
         nc.vector.tensor_copy(v_listed[0][:], v_pools[0][:].indirect(offsets[:]))
         nc.vector.tensor_reduce(neg_max[:], scores[:], AXIS.X, ALU.max, negate=True)
         nc.vector.tensor_copy(v_listed[1][:], v_pools[1][:].indirect(offsets[:]))
         score_planes = scores[:].rearrange("q (s t) -> q t s", t=PACK)
+        probs_turned = ps.tile([P, PACK, NQ], F32, name="probs_turned")
         for half in range(2):
             planes = slice(2 * half, 2 * half + 2)
             nc.scalar.activation(
@@ -137,15 +132,16 @@ def tile_attend_soft_topk_kernel(tc, qT, k_words, k_scales, vT, vs, offs, out):
                 bias=neg_max[:],
                 accum_out=half_total[:, half : half + 1],
             )
-
-        v_codes = [late.tile([P, P], U32, name=f"v_codes{h}", align_bytes=64, offset=V1_AT + 1024 + 512 * h) for h in range(V_BLOCKS)]
-        inv_total = late.tile([P, 1], F32, name="inv_total", align_bytes=64, offset=V1_AT + 2048)
+        v_codes = [
+            late.tile([P, P], U32, name="v_codes0", align_bytes=64, offset=V1_AT + 512),
+            sb.tile([P, P], U32, name="v_codes1", align_bytes=64),
+        ]
+        inv_total = late.tile([P, 1], F32, name="inv_total", align_bytes=64, offset=V1_AT + 1024)
         v_scales = [sb.tile([P, P], U8, name=f"v_scales{h}", align_bytes=64) for h in range(V_BLOCKS)]
         v_bf = [sb.tile([P, P, PACK], BF16, name=f"v_bf{h}", align_bytes=64) for h in range(V_BLOCKS)]
-        probs_turned = ps.tile([P, PACK, NQ], F32, name="probs_turned")
 
         def turn_values(h):
-            v_turned = (ps.tile([P, 2, P], F32, name="v_turned0") if h == 0 else shared_bank.tile([P, 2, P], F32, name="v_turned1", offset=0))
+            v_turned = ps.tile([P, 2, P], F32, name="v_turned0") if h == 0 else shared_bank.tile([P, 2, P], F32, name="v_turned1", offset=0)
             words = v_listed[h][:].bitcast(F32)
             for u in range(2):
                 nc.tensor.transpose(v_turned[:, u, :], words[:, u : 2 * P : 2], identity[:])
@@ -158,9 +154,9 @@ def tile_attend_soft_topk_kernel(tc, qT, k_words, k_scales, vT, vs, offs, out):
         for t in range(PACK):
             nc.tensor.transpose(probs_turned[:, t, :], probs[:, t, :], identity[:])
         nc.scalar.activation(total[:], half_total[:, 0:1], ACT.Identity, bias=half_total[:, 1:2])
-        turn_values(1)
 
-        w_bf = late.tile([P, NQ, PACK], BF16, name="w_bf", align_bytes=64, offset=V1_AT)
+        turn_values(1)
+        w_bf = late.tile([P, NQ, PACK], BF16, name="w_bf", align_bytes=64, offset=V1_AT + 2048)
         w_codes = sb.tile([P, NQ], U32, name="w_codes", align_bytes=64)
         w_scales = sb.tile([P, NQ], U8, name="w_scales", align_bytes=64)
         nc.vector.tensor_tensor(
@@ -171,8 +167,8 @@ def tile_attend_soft_topk_kernel(tc, qT, k_words, k_scales, vT, vs, offs, out):
         )
         quantise_values(0)
         nc.vector.quantize_mx(w_codes[:].bitcast(FP8X4), w_scales[:], w_bf[:].rearrange("p q t -> p (q t)"))
-        quantise_values(1)
         nc.vector.reciprocal(inv_total[:], total[:])
+        quantise_values(1)
 
         for h in range(V_BLOCKS):
             cols = slice(h * P, (h + 1) * P)

@@ -35,12 +35,13 @@ def tile_attend_soft_topk_kernel(tc, qT, k_words, k_scales, vT, vs, offs, out):
 
         V0_AT, V1_AT, Q0_AT, Q1_AT = 0, 8192, 16384, 18432
         SCALES_FROM = 96
+        V_AHEAD = T // 2
 
         offsets = sb.tile([P, N // 16], U16, name="offsets")
         key_pool = sb.tile([P, T], I32, name="key_pool", align_bytes=64)
         key_scales = sb.tile([P, PASSES, N], U8, name="key_scales", align_bytes=64)
         identity = sb.tile([P, P], F32, name="identity", align_bytes=64)
-        scale_pool = late.tile([P, T], U8, name="scale_pool", align_bytes=64, offset=V1_AT - T // 2)
+        scale_pool = late.tile([P, T], U8, name="scale_pool", align_bytes=64, offset=V1_AT + 4096)
         vs_pool = sb.tile([P, T], F32, name="vs_pool", align_bytes=64)
         q_raw = [late.tile([P, PACK, NQ], F32, name=f"q_raw{o}", align_bytes=64, offset=at) for o, at in enumerate((Q0_AT, Q1_AT))]
         v_pools = [late.tile([P, T], F32, name=f"v_pool{h}", align_bytes=64, offset=at) for h, at in enumerate((V0_AT, V1_AT))]
@@ -57,14 +58,15 @@ def tile_attend_soft_topk_kernel(tc, qT, k_words, k_scales, vT, vs, offs, out):
         nc.sync.dma_start(key_pool[:], k_words[0].rearrange("p t b -> p (t b)").bitcast(I32))
         for o in range(PASSES):
             nc.sync.dma_start(q_raw[o][:], q_rows[o])
+        nc.sync.dma_start(v_pools[0][:, 0:V_AHEAD], vT[0:P, 0:V_AHEAD])
 
         listed_scales = sb.tile([P, N], U8, name="listed_scales", align_bytes=64)
         nc.vector.tensor_copy(listed_scales[:], scale_pool[:].indirect(offsets[:]))
         for a in range(4):
             rows = slice(SCALES_FROM + 8 * a, SCALES_FROM + 8 * a + 8)
             nc.sync.dma_start(key_scales[32 * a : 32 * a + 4, :, :].bitcast(I32), listed_scales[rows, :].bitcast(I32))
-        for h in range(V_BLOCKS):
-            nc.sync.dma_start(v_pools[h][:], vT[h * P : (h + 1) * P, :])
+        nc.sync.dma_start(v_pools[0][:, V_AHEAD:T], vT[0:P, V_AHEAD:T])
+        nc.sync.dma_start(v_pools[1][:], vT[P:DV, :])
 
         vs_listed = sb.tile([P, N], F32, name="vs_listed", align_bytes=64)
         nc.vector.tensor_copy(vs_listed[:], vs_pool[:].indirect(offsets[:]))

@@ -33,9 +33,11 @@ def tile_attend_soft_topk_kernel(tc, qT, k_words, k_scales, vT, vs, offs, out):
         ps = ctx.enter_context(tc.psum_pool(name="ps", bufs=1))
         shared_bank = ctx.enter_context(tc.psum_pool(name="shared_bank", bufs=1))
 
-        V0_AT, V1_AT, Q0_AT, Q1_AT = 0, 8192, 16384, 18432
+        V0_AT, V1_AT, Q0_AT, Q1_AT = 0, 8192, 16384, 20480
         SCALES_FROM = 96
-        V_AHEAD = T // 2
+        QC1_AT = 24576
+        V_AHEAD = 3 * T // 8
+        K_AHEAD = T // 8
 
         offsets = sb.tile([P, N // 16], U16, name="offsets")
         key_pool = sb.tile([P, T], I32, name="key_pool", align_bytes=64)
@@ -52,10 +54,12 @@ def tile_attend_soft_topk_kernel(tc, qT, k_words, k_scales, vT, vs, offs, out):
         make_identity(nc, identity[:])
 
         q_rows = qT[0].rearrange("(o p j) q -> o p j q", o=PASSES, j=PACK)
+        key_rows = k_words[0].rearrange("p t b -> p (t b)").bitcast(I32)
+        nc.sync.dma_start(key_pool[:, 0:K_AHEAD], key_rows[:, 0:K_AHEAD])
         nc.sync.dma_start(offsets[:], offs)
         nc.sync.dma_start(scale_pool[SCALES_FROM:P, :].bitcast(I32), k_scales.bitcast(I32).rearrange("o f t -> f o t"))
+        nc.sync.dma_start(key_pool[:, K_AHEAD:T], key_rows[:, K_AHEAD:T])
         nc.sync.dma_start(vs_pool[VS_ROW : VS_ROW + 1, :], vs[0:1, :])
-        nc.sync.dma_start(key_pool[:], k_words[0].rearrange("p t b -> p (t b)").bitcast(I32))
         for o in range(PASSES):
             nc.sync.dma_start(q_raw[o][:], q_rows[o])
         nc.sync.dma_start(v_pools[0][:, 0:V_AHEAD], vT[0:P, 0:V_AHEAD])
@@ -68,22 +72,14 @@ def tile_attend_soft_topk_kernel(tc, qT, k_words, k_scales, vT, vs, offs, out):
         nc.sync.dma_start(v_pools[0][:, V_AHEAD:T], vT[0:P, V_AHEAD:T])
         nc.sync.dma_start(v_pools[1][:], vT[P:DV, :])
 
-        vs_listed = sb.tile([P, N], F32, name="vs_listed", align_bytes=64)
-        nc.vector.tensor_copy(vs_listed[:], vs_pool[:].indirect(offsets[:]))
-        vs_turned = ps.tile([P, PACK, P], F32, name="vs_turned")
-        for t in range(PACK):
-            nc.tensor.transpose(vs_turned[:, t, :], vs_listed[:, t:N:PACK], identity[:])
-
         q_bf = [sb.tile([P, NQ, PACK], BF16, name=f"q_bf{o}", align_bytes=64) for o in range(PASSES)]
         q_codes = [
             sb.tile([P, NQ], U32, name="q_codes0", align_bytes=64),
-            sb.tile([P, NQ], U32, name="q_codes1", align_bytes=64),
+            late.tile([P, NQ], U32, name="q_codes1", align_bytes=64, offset=QC1_AT),
         ]
         q_scales = [sb.tile([P, NQ], U8, name=f"q_scales{o}", align_bytes=64) for o in range(PASSES)]
         for o in range(PASSES):
             nc.scalar.activation(q_bf[o][:], q_raw[o][:].rearrange("p j q -> p q j"), ACT.Copy)
-        vs_slot = late.tile([P, PACK], F32, name="vs_slot", align_bytes=64, offset=Q1_AT)
-        nc.scalar.activation(vs_slot[:], vs_turned[:, :, VS_ROW], ACT.Copy)
 
         def quantise_queries(o):
             nc.vector.quantize_mx(q_codes[o][:].bitcast(FP8X4), q_scales[o][:], q_bf[o][:].rearrange("p q j -> p (q j)"))
@@ -99,6 +95,8 @@ def tile_attend_soft_topk_kernel(tc, qT, k_words, k_scales, vT, vs, offs, out):
         for o in range(PASSES):
             nc.vector.tensor_copy(key_words[o][:].bitcast(U16), halves[:, o, :])
         quantise_queries(1)
+        vs_listed = late.tile([P, N], F32, name="vs_listed", align_bytes=64, offset=Q1_AT - 1536)
+        nc.vector.tensor_copy(vs_listed[:], vs_pool[:].indirect(offsets[:]))
 
         scores = shared_bank.tile([P, N], F32, name="scores", offset=0)
         for o in range(PASSES):
@@ -112,16 +110,23 @@ def tile_attend_soft_topk_kernel(tc, qT, k_words, k_scales, vT, vs, offs, out):
                 stop=(o == PASSES - 1),
             )
 
-        neg_max = late.tile([P, 1], F32, name="neg_max", align_bytes=64, offset=V0_AT)
+        vs_planes = late.tile([P, PACK, P], F32, name="vs_planes", align_bytes=64, offset=Q1_AT + 1024)
+        vs_turned = ps.tile([P, PACK, P], F32, name="vs_turned")
+        vs_slot = sb.tile([P, PACK], F32, name="vs_slot", align_bytes=64)
+        nc.scalar.activation(vs_planes[:].rearrange("p t s -> p s t"), vs_listed[:].rearrange("p (s t) -> p s t", t=PACK), ACT.Copy)
+        for t in range(PACK):
+            nc.tensor.transpose(vs_turned[:, t, :], vs_planes[:, t, :], identity[:])
+
+        neg_max = sb.tile([P, 1], F32, name="neg_max", align_bytes=64)
         half_total = sb.tile([P, 2], F32, name="half_total")
         total = sb.tile([P, 1], F32, name="total")
         probs = sb.tile([P, PACK, P], F32, name="probs", align_bytes=64)
         v_listed = [
-            sb.tile([P, N], BF16, name="v_listed0", align_bytes=64),
+            late.tile([P, N], BF16, name="v_listed0", align_bytes=64, offset=QC1_AT),
             sb.tile([P, N], BF16, name="v_listed1", align_bytes=64),
         ]
-        nc.vector.tensor_copy(v_listed[0][:], v_pools[0][:].indirect(offsets[:]))
         nc.vector.tensor_reduce(neg_max[:], scores[:], AXIS.X, ALU.max, negate=True)
+        nc.vector.tensor_copy(v_listed[0][:], v_pools[0][:].indirect(offsets[:]))
         nc.vector.tensor_copy(v_listed[1][:], v_pools[1][:].indirect(offsets[:]))
         score_planes = scores[:].rearrange("q (s t) -> q t s", t=PACK)
         probs_turned = ps.tile([P, PACK, NQ], F32, name="probs_turned")
@@ -152,10 +157,11 @@ def tile_attend_soft_topk_kernel(tc, qT, k_words, k_scales, vT, vs, offs, out):
         def quantise_values(h):
             nc.vector.quantize_mx(v_codes[h][:].bitcast(FP8X4), v_scales[h][:], v_bf[h][:].rearrange("p e t -> p (e t)"))
 
-        turn_values(0)
         for t in range(PACK):
             nc.tensor.transpose(probs_turned[:, t, :], probs[:, t, :], identity[:])
+        nc.scalar.activation(vs_slot[:], vs_turned[:, :, VS_ROW], ACT.Copy)
         nc.scalar.activation(total[:], half_total[:, 0:1], ACT.Identity, bias=half_total[:, 1:2])
+        turn_values(0)
 
         turn_values(1)
         w_bf = late.tile([P, NQ, PACK], BF16, name="w_bf", align_bytes=64, offset=V1_AT + 2048)
@@ -169,8 +175,8 @@ def tile_attend_soft_topk_kernel(tc, qT, k_words, k_scales, vT, vs, offs, out):
         )
         quantise_values(0)
         nc.vector.quantize_mx(w_codes[:].bitcast(FP8X4), w_scales[:], w_bf[:].rearrange("p q t -> p (q t)"))
-        nc.vector.reciprocal(inv_total[:], total[:])
         quantise_values(1)
+        nc.vector.reciprocal(inv_total[:], total[:])
 
         for h in range(V_BLOCKS):
             cols = slice(h * P, (h + 1) * P)

@@ -79,7 +79,11 @@ def tile_attend_soft_topk_kernel(tc, qT, k_words, k_scales, vT, vs, offs, out):
         ]
         q_scales = [sb.tile([P, NQ], U8, name=f"q_scales{o}", align_bytes=64) for o in range(PASSES)]
         for o in range(PASSES):
-            nc.scalar.activation(q_bf[o][:], q_raw[o][:].rearrange("p j q -> p q j"), ACT.Copy)
+            nc.scalar.activation(
+                q_bf[o][:].rearrange("p (c i) j -> p c j i", i=4),
+                q_raw[o][:].rearrange("p j (c i) -> p c j i", i=4),
+                ACT.Copy,
+            )
 
         def quantise_queries(o):
             nc.vector.quantize_mx(q_codes[o][:].bitcast(FP8X4), q_scales[o][:], q_bf[o][:].rearrange("p q j -> p (q j)"))
@@ -113,7 +117,10 @@ def tile_attend_soft_topk_kernel(tc, qT, k_words, k_scales, vT, vs, offs, out):
         vs_planes = late.tile([P, PACK, P], F32, name="vs_planes", align_bytes=64, offset=Q1_AT + 1024)
         vs_turned = ps.tile([P, PACK, P], F32, name="vs_turned")
         vs_slot = sb.tile([P, PACK], F32, name="vs_slot", align_bytes=64)
-        nc.scalar.activation(vs_planes[:].rearrange("p t s -> p s t"), vs_listed[:].rearrange("p (s t) -> p s t", t=PACK), ACT.Copy)
+        nc.scalar.copy(
+            vs_planes[:].rearrange("p (u c) (b j) -> p b u j c", c=2, j=8),
+            vs_listed[:].rearrange("p (b u j c) -> p b u j c", u=2, j=8, c=2),
+        )
         for t in range(PACK):
             nc.tensor.transpose(vs_turned[:, t, :], vs_planes[:, t, :], identity[:])
 
@@ -126,15 +133,15 @@ def tile_attend_soft_topk_kernel(tc, qT, k_words, k_scales, vT, vs, offs, out):
             sb.tile([P, N], BF16, name="v_listed1", align_bytes=64),
         ]
         nc.vector.tensor_reduce(neg_max[:], scores[:], AXIS.X, ALU.max, negate=True)
-        nc.vector.tensor_copy(v_listed[0][:], v_pools[0][:].indirect(offsets[:]))
-        nc.vector.tensor_copy(v_listed[1][:], v_pools[1][:].indirect(offsets[:]))
-        score_planes = scores[:].rearrange("q (s t) -> q t s", t=PACK)
+        nc.vector.tensor_copy(v_listed[0][:].rearrange("p (u b i) -> p b u i", u=2, i=16), v_pools[0][:].indirect(offsets[:]))
+        nc.vector.tensor_copy(v_listed[1][:].rearrange("p (u b i) -> p b u i", u=2, i=16), v_pools[1][:].indirect(offsets[:]))
+        score_planes = scores[:].rearrange("q (b u j c) -> q u c b j", u=2, j=8, c=2)
         probs_turned = ps.tile([P, PACK, NQ], F32, name="probs_turned")
         for half in range(2):
             planes = slice(2 * half, 2 * half + 2)
             nc.scalar.activation(
-                probs[:, planes, :],
-                score_planes[:, planes, :],
+                probs[:, planes, :].rearrange("q c (b j) -> q c b j", j=8),
+                score_planes[:, half],
                 ACT.Exp,
                 bias=neg_max[:],
                 accum_out=half_total[:, half : half + 1],
@@ -151,7 +158,7 @@ def tile_attend_soft_topk_kernel(tc, qT, k_words, k_scales, vT, vs, offs, out):
             v_turned = ps.tile([P, 2, P], F32, name="v_turned0") if h == 0 else shared_bank.tile([P, 2, P], F32, name="v_turned1", offset=0)
             words = v_listed[h][:].bitcast(F32)
             for u in range(2):
-                nc.tensor.transpose(v_turned[:, u, :], words[:, u : 2 * P : 2], identity[:])
+                nc.tensor.transpose(v_turned[:, u, :], words[:, u * P : (u + 1) * P], identity[:])
             nc.scalar.copy(v_bf[h][:].bitcast(F32), v_turned[:].rearrange("p u e -> p e u"))
 
         def quantise_values(h):

@@ -37,7 +37,6 @@ def tile_attend_soft_topk_kernel(tc, qT, k_words, k_scales, vT, vs, offs, out):
         SCALES_FROM = 96
         QC1_AT = 24576
         V_AHEAD = 3 * T // 8
-        K_AHEAD = T // 8
 
         offsets = sb.tile([P, N // 16], U16, name="offsets")
         key_pool = sb.tile([P, T], I32, name="key_pool", align_bytes=64)
@@ -54,11 +53,9 @@ def tile_attend_soft_topk_kernel(tc, qT, k_words, k_scales, vT, vs, offs, out):
         make_identity(nc, identity[:])
 
         q_rows = qT[0].rearrange("(o p j) q -> o p j q", o=PASSES, j=PACK)
-        key_rows = k_words[0].rearrange("p t b -> p (t b)").bitcast(I32)
-        nc.sync.dma_start(key_pool[:, 0:K_AHEAD], key_rows[:, 0:K_AHEAD])
-        nc.sync.dma_start(offsets[:], offs)
         nc.sync.dma_start(scale_pool[SCALES_FROM:P, :].bitcast(I32), k_scales.bitcast(I32).rearrange("o f t -> f o t"))
-        nc.sync.dma_start(key_pool[:, K_AHEAD:T], key_rows[:, K_AHEAD:T])
+        nc.sync.dma_start(offsets[:], offs)
+        nc.sync.dma_start(key_pool[:], k_words[0].rearrange("p t b -> p (t b)").bitcast(I32))
         nc.sync.dma_start(vs_pool[VS_ROW : VS_ROW + 1, :], vs[0:1, :])
         for o in range(PASSES):
             nc.sync.dma_start(q_raw[o][:], q_rows[o])

@@ -36,6 +36,7 @@ def tile_attend_soft_topk_kernel(tc, qT, k_words, k_scales, vT, vs, offs, out):
         V0_AT, V1_AT, Q0_AT, Q1_AT = 0, 8192, 16384, 20480
         SCALES_FROM = 96
         QC1_AT = 24576
+        CHAIN_AT = 26624
         V_AHEAD = 3 * T // 8
 
         offsets = sb.tile([P, N // 16], U16, name="offsets")
@@ -112,8 +113,7 @@ def tile_attend_soft_topk_kernel(tc, qT, k_words, k_scales, vT, vs, offs, out):
             )
 
         vs_planes = late.tile([P, PACK, P], F32, name="vs_planes", align_bytes=64, offset=Q1_AT + 1024)
-        vs_turned = ps.tile([P, PACK, P], F32, name="vs_turned")
-        vs_slot = sb.tile([P, PACK], F32, name="vs_slot", align_bytes=64)
+        vs_turned = shared_bank.tile([P, PACK, P], F32, name="vs_turned", offset=2048)
         nc.scalar.copy(
             vs_planes[:].rearrange("p (u c) (b j) -> p b u j c", c=2, j=8),
             vs_listed[:].rearrange("p (b u j c) -> p b u j c", u=2, j=8, c=2),
@@ -121,7 +121,8 @@ def tile_attend_soft_topk_kernel(tc, qT, k_words, k_scales, vT, vs, offs, out):
         for t in range(PACK):
             nc.tensor.transpose(vs_turned[:, t, :], vs_planes[:, t, :], identity[:])
 
-        neg_max = sb.tile([P, 1], F32, name="neg_max", align_bytes=64)
+        neg_max = late.tile([P, 1], F32, name="neg_max", align_bytes=64, offset=CHAIN_AT)
+        vs_slot = late.tile([P, PACK], F32, name="vs_slot", align_bytes=64, offset=CHAIN_AT)
         half_total = sb.tile([P, 2], F32, name="half_total")
         total = sb.tile([P, 1], F32, name="total")
         probs = sb.tile([P, PACK, P], F32, name="probs", align_bytes=64)
@@ -151,23 +152,27 @@ def tile_attend_soft_topk_kernel(tc, qT, k_words, k_scales, vT, vs, offs, out):
         v_scales = [sb.tile([P, P], U8, name=f"v_scales{h}", align_bytes=64) for h in range(V_BLOCKS)]
         v_bf = [sb.tile([P, P, PACK], BF16, name=f"v_bf{h}", align_bytes=64) for h in range(V_BLOCKS)]
 
-        def turn_values(h):
-            v_turned = ps.tile([P, 2, P], F32, name="v_turned0") if h == 0 else shared_bank.tile([P, 2, P], F32, name="v_turned1", offset=0)
+        def turn_values(h, parts):
+            v_turned = shared_bank.tile([P, 2, P], F32, name=f"v_turned{h}", offset=2048 * (1 - h))
             words = v_listed[h][:].bitcast(F32)
             for u in range(2):
                 nc.tensor.transpose(v_turned[:, u, :], words[:, u * P : (u + 1) * P], identity[:])
-            nc.scalar.copy(v_bf[h][:].bitcast(F32), v_turned[:].rearrange("p u e -> p e u"))
+            for part in parts:
+                nc.scalar.copy(v_bf[h][:, part, :].bitcast(F32), v_turned[:, :, part].rearrange("p u e -> p e u"))
 
-        def quantise_values(h):
-            nc.vector.quantize_mx(v_codes[h][:].bitcast(FP8X4), v_scales[h][:], v_bf[h][:].rearrange("p e t -> p (e t)"))
+        def quantise_values(h, parts):
+            for part in parts:
+                nc.vector.quantize_mx(
+                    v_codes[h][:, part].bitcast(FP8X4), v_scales[h][:, part], v_bf[h][:, part, :].rearrange("p e t -> p (e t)")
+                )
 
+        whole, halved = [slice(0, P)], [slice(0, P // 2), slice(P // 2, P)]
         for t in range(PACK):
             nc.tensor.transpose(probs_turned[:, t, :], probs[:, t, :], identity[:])
         nc.scalar.activation(vs_slot[:], vs_turned[:, :, VS_ROW], ACT.Copy)
         nc.scalar.activation(total[:], half_total[:, 0:1], ACT.Identity, bias=half_total[:, 1:2])
-        turn_values(0)
+        turn_values(0, whole)
 
-        turn_values(1)
         w_bf = late.tile([P, NQ, PACK], BF16, name="w_bf", align_bytes=64, offset=V1_AT + 2048)
         w_codes = sb.tile([P, NQ], U32, name="w_codes", align_bytes=64)
         w_scales = sb.tile([P, NQ], U8, name="w_scales", align_bytes=64)
@@ -177,9 +182,10 @@ def tile_attend_soft_topk_kernel(tc, qT, k_words, k_scales, vT, vs, offs, out):
             vs_slot[:].unsqueeze(1).to_broadcast([P, NQ, PACK]),
             ALU.mult,
         )
-        quantise_values(0)
+        turn_values(1, halved)
+        quantise_values(0, whole)
         nc.vector.quantize_mx(w_codes[:].bitcast(FP8X4), w_scales[:], w_bf[:].rearrange("p q t -> p (q t)"))
-        quantise_values(1)
+        quantise_values(1, halved)
         nc.vector.reciprocal(inv_total[:], total[:])
 
         for h in range(V_BLOCKS):

@@ -184,9 +184,9 @@ def tile_attend_soft_topk_kernel(tc, qT, k_words, k_scales, vT, vs, offs, out):
         )
         turn_values(1, halved)
         quantise_values(0, whole)
+        nc.vector.reciprocal(inv_total[:], total[:])
         nc.vector.quantize_mx(w_codes[:].bitcast(FP8X4), w_scales[:], w_bf[:].rearrange("p q t -> p (q t)"))
         quantise_values(1, halved)
-        nc.vector.reciprocal(inv_total[:], total[:])
 
         for h in range(V_BLOCKS):
             cols = slice(h * P, (h + 1) * P)

@@ -20,7 +20,11 @@ PACK = 4
 N, T, D, DV, NQ = 512, 2048, 1024, 256, 128
 PASSES = D // (P * PACK)
 V_BLOCKS = DV // P
-VS_ROW = 127
+BANK = 2048
+VS_ROW = P - 1
+SCALES_FROM = 96
+V_AHEAD = 3 * T // 8
+ON_VECTOR = 288
 
 FLOPS = 2 * NQ * N * (D + DV)
 
@@ -29,24 +33,20 @@ def tile_attend_soft_topk_kernel(tc, qT, k_words, k_scales, vT, vs, offs, out):
     nc = tc.nc
     with ExitStack() as ctx:
         sb = ctx.enter_context(tc.tile_pool(name="sb", bufs=1))
-        late = ctx.enter_context(tc.tile_pool(name="late", bufs=1))
+        placed = ctx.enter_context(tc.tile_pool(name="placed", bufs=1))
         ps = ctx.enter_context(tc.psum_pool(name="ps", bufs=1))
-        shared_bank = ctx.enter_context(tc.psum_pool(name="shared_bank", bufs=1))
+        banks = ctx.enter_context(tc.psum_pool(name="banks", bufs=1))
 
-        V0_AT, V1_AT, Q0_AT, Q1_AT = 0, 8192, 16384, 20480
-        SCALES_FROM = 96
-        QC1_AT = 24576
-        CHAIN_AT = 26624
-        V_AHEAD = 3 * T // 8
+        V0_AT, V1_AT, Q0_AT, Q1_AT, QC1_AT = 0, 8192, 16384, 18432, 20480
 
         offsets = sb.tile([P, N // 16], U16, name="offsets")
         key_pool = sb.tile([P, T], I32, name="key_pool", align_bytes=64)
         key_scales = sb.tile([P, PASSES, N], U8, name="key_scales", align_bytes=64)
         identity = sb.tile([P, P], F32, name="identity", align_bytes=64)
-        scale_pool = late.tile([P, T], U8, name="scale_pool", align_bytes=64, offset=V1_AT + 4096)
+        scale_pool = placed.tile([P, T], U8, name="scale_pool", align_bytes=64, offset=V1_AT)
         vs_pool = sb.tile([P, T], F32, name="vs_pool", align_bytes=64)
-        q_raw = [late.tile([P, PACK, NQ], F32, name=f"q_raw{o}", align_bytes=64, offset=at) for o, at in enumerate((Q0_AT, Q1_AT))]
-        v_pools = [late.tile([P, T], F32, name=f"v_pool{h}", align_bytes=64, offset=at) for h, at in enumerate((V0_AT, V1_AT))]
+        q_raw = [placed.tile([P, PACK, NQ], F32, name=f"q_raw{o}", align_bytes=64, offset=at) for o, at in enumerate((Q0_AT, Q1_AT))]
+        v_pools = [placed.tile([P, T], F32, name=f"v_pool{h}", align_bytes=64, offset=at) for h, at in enumerate((V0_AT, V1_AT))]
 
         nc.vector.memset(scale_pool[0:SCALES_FROM, :].bitcast(I32), 0)
         nc.vector.memset(key_scales[:].rearrange("p o i -> p (o i)").bitcast(I32), 0)
@@ -56,8 +56,8 @@ def tile_attend_soft_topk_kernel(tc, qT, k_words, k_scales, vT, vs, offs, out):
         q_rows = qT[0].rearrange("(o p j) q -> o p j q", o=PASSES, j=PACK)
         nc.sync.dma_start(scale_pool[SCALES_FROM:P, :].bitcast(I32), k_scales.bitcast(I32).rearrange("o f t -> f o t"))
         nc.sync.dma_start(offsets[:], offs)
-        nc.sync.dma_start(key_pool[:], k_words[0].rearrange("p t b -> p (t b)").bitcast(I32))
         nc.sync.dma_start(vs_pool[VS_ROW : VS_ROW + 1, :], vs[0:1, :])
+        nc.sync.dma_start(key_pool[:], k_words[0].rearrange("p t b -> p (t b)").bitcast(I32))
         for o in range(PASSES):
             nc.sync.dma_start(q_raw[o][:], q_rows[o])
         nc.sync.dma_start(v_pools[0][:, 0:V_AHEAD], vT[0:P, 0:V_AHEAD])
@@ -70,10 +70,17 @@ def tile_attend_soft_topk_kernel(tc, qT, k_words, k_scales, vT, vs, offs, out):
         nc.sync.dma_start(v_pools[0][:, V_AHEAD:T], vT[0:P, V_AHEAD:T])
         nc.sync.dma_start(v_pools[1][:], vT[P:DV, :])
 
+        vs_listed = sb.tile([P, N], F32, name="vs_listed", align_bytes=64)
+        vs_turned = banks.tile([P, PACK, P], F32, name="vs_turned", offset=BANK)
+        vs_slot = sb.tile([P, PACK], F32, name="vs_slot", align_bytes=64)
+        nc.scalar.activation(vs_listed[:], vs_pool[:].indirect(offsets[:]), ACT.Copy)
+        for t in range(PACK):
+            nc.tensor.transpose(vs_turned[:, t, :], vs_listed[:, t:N:PACK], identity[:])
+
         q_bf = [sb.tile([P, NQ, PACK], BF16, name=f"q_bf{o}", align_bytes=64) for o in range(PASSES)]
         q_codes = [
             sb.tile([P, NQ], U32, name="q_codes0", align_bytes=64),
-            late.tile([P, NQ], U32, name="q_codes1", align_bytes=64, offset=QC1_AT),
+            placed.tile([P, NQ], U32, name="q_codes1", align_bytes=64, offset=QC1_AT),
         ]
         q_scales = [sb.tile([P, NQ], U8, name=f"q_scales{o}", align_bytes=64) for o in range(PASSES)]
         for o in range(PASSES):
@@ -82,25 +89,21 @@ def tile_attend_soft_topk_kernel(tc, qT, k_words, k_scales, vT, vs, offs, out):
                 q_raw[o][:].rearrange("p j (c i) -> p c j i", i=4),
                 ACT.Copy,
             )
+        nc.scalar.activation(vs_slot[:], vs_turned[:, :, VS_ROW], ACT.Copy)
 
         def quantise_queries(o):
             nc.vector.quantize_mx(q_codes[o][:].bitcast(FP8X4), q_scales[o][:], q_bf[o][:].rearrange("p q j -> p (q j)"))
 
         key_pairs = sb.tile([P, N], U32, name="key_pairs", align_bytes=64)
-        key_words = [
-            late.tile([P, 2 * N], U8, name="key_words0", align_bytes=64, offset=Q0_AT),
-            late.tile([P, 2 * N], U8, name="key_words1", align_bytes=64, offset=Q1_AT + 1024),
-        ]
+        key_words = [placed.tile([P, 2 * N], U8, name=f"key_words{o}", align_bytes=64, offset=at) for o, at in enumerate((Q0_AT, Q1_AT))]
         nc.vector.tensor_copy(key_pairs[:], key_pool[:].bitcast(U32).indirect(offsets[:]))
         halves = key_pairs[:].bitcast(U16).rearrange("p (i o) -> p o i", o=PASSES)
         quantise_queries(0)
         for o in range(PASSES):
             nc.vector.tensor_copy(key_words[o][:].bitcast(U16), halves[:, o, :])
         quantise_queries(1)
-        vs_listed = late.tile([P, N], F32, name="vs_listed", align_bytes=64, offset=Q1_AT - 1536)
-        nc.vector.tensor_copy(vs_listed[:], vs_pool[:].indirect(offsets[:]))
 
-        scores = shared_bank.tile([P, N], F32, name="scores", offset=0)
+        scores = banks.tile([P, N], F32, name="scores", offset=0)
         for o in range(PASSES):
             nc.tensor.matmul_mx(
                 scores[:],
@@ -112,51 +115,44 @@ def tile_attend_soft_topk_kernel(tc, qT, k_words, k_scales, vT, vs, offs, out):
                 stop=(o == PASSES - 1),
             )
 
-        vs_planes = late.tile([P, PACK, P], F32, name="vs_planes", align_bytes=64, offset=Q1_AT + 1024)
-        vs_turned = shared_bank.tile([P, PACK, P], F32, name="vs_turned", offset=2048)
-        nc.scalar.copy(
-            vs_planes[:].rearrange("p (u c) (b j) -> p b u j c", c=2, j=8),
-            vs_listed[:].rearrange("p (b u j c) -> p b u j c", u=2, j=8, c=2),
-        )
-        for t in range(PACK):
-            nc.tensor.transpose(vs_turned[:, t, :], vs_planes[:, t, :], identity[:])
-
-        neg_max = late.tile([P, 1], F32, name="neg_max", align_bytes=64, offset=CHAIN_AT)
-        vs_slot = late.tile([P, PACK], F32, name="vs_slot", align_bytes=64, offset=CHAIN_AT)
+        neg_max = sb.tile([P, 1], F32, name="neg_max", align_bytes=64)
         half_total = sb.tile([P, 2], F32, name="half_total")
         total = sb.tile([P, 1], F32, name="total")
         probs = sb.tile([P, PACK, P], F32, name="probs", align_bytes=64)
         v_listed = [
-            late.tile([P, N], BF16, name="v_listed0", align_bytes=64, offset=QC1_AT),
+            placed.tile([P, N], BF16, name="v_listed0", align_bytes=64, offset=QC1_AT),
             sb.tile([P, N], BF16, name="v_listed1", align_bytes=64),
         ]
         nc.vector.tensor_reduce(neg_max[:], scores[:], AXIS.X, ALU.max, negate=True)
-        nc.vector.tensor_copy(v_listed[0][:].rearrange("p (u b i) -> p b u i", u=2, i=16), v_pools[0][:].indirect(offsets[:]))
-        nc.vector.tensor_copy(v_listed[1][:].rearrange("p (u b i) -> p b u i", u=2, i=16), v_pools[1][:].indirect(offsets[:]))
-        score_planes = scores[:].rearrange("q (b u j c) -> q u c b j", u=2, j=8, c=2)
+        nc.vector.tensor_copy(v_listed[0][:], v_pools[0][:].indirect(offsets[:]))
+        score_planes = scores[:].rearrange("q (s t) -> q t s", t=PACK)
         probs_turned = ps.tile([P, PACK, NQ], F32, name="probs_turned")
         for half in range(2):
             planes = slice(2 * half, 2 * half + 2)
             nc.scalar.activation(
-                probs[:, planes, :].rearrange("q c (b j) -> q c b j", j=8),
-                score_planes[:, half],
-                ACT.Exp,
-                bias=neg_max[:],
-                accum_out=half_total[:, half : half + 1],
+                probs[:, planes, :], score_planes[:, planes, :], ACT.Exp, bias=neg_max[:], accum_out=half_total[:, half : half + 1]
             )
+        nc.scalar.activation(total[:], half_total[:, 0:1], ACT.Identity, bias=half_total[:, 1:2])
+        cut = ON_VECTOR // 16
+        nc.vector.tensor_copy(v_listed[1][:, 0:ON_VECTOR], v_pools[1][:].indirect(offsets[:, 0:cut]))
+        nc.scalar.activation(v_listed[1][:, ON_VECTOR:N], v_pools[1][:].indirect(offsets[:, cut : N // 16]), ACT.Copy)
+
         v_codes = [
-            late.tile([P, P], U32, name="v_codes0", align_bytes=64, offset=V1_AT + 512),
+            placed.tile([P, P], U32, name="v_codes0", align_bytes=64, offset=V1_AT + 512),
             sb.tile([P, P], U32, name="v_codes1", align_bytes=64),
         ]
-        inv_total = late.tile([P, 1], F32, name="inv_total", align_bytes=64, offset=V1_AT + 1024)
+        inv_total = placed.tile([P, 1], F32, name="inv_total", align_bytes=64, offset=V1_AT + 1024)
         v_scales = [sb.tile([P, P], U8, name=f"v_scales{h}", align_bytes=64) for h in range(V_BLOCKS)]
-        v_bf = [sb.tile([P, P, PACK], BF16, name=f"v_bf{h}", align_bytes=64) for h in range(V_BLOCKS)]
+        v_bf = [
+            placed.tile([P, P, PACK], BF16, name="v_bf0", align_bytes=64, offset=V1_AT + 4096),
+            sb.tile([P, P, PACK], BF16, name="v_bf1", align_bytes=64),
+        ]
 
         def turn_values(h, parts):
-            v_turned = shared_bank.tile([P, 2, P], F32, name=f"v_turned{h}", offset=2048 * (1 - h))
+            v_turned = banks.tile([P, 2, P], F32, name=f"v_turned{h}", offset=BANK * h)
             words = v_listed[h][:].bitcast(F32)
             for u in range(2):
-                nc.tensor.transpose(v_turned[:, u, :], words[:, u * P : (u + 1) * P], identity[:])
+                nc.tensor.transpose(v_turned[:, u, :], words[:, u : N // 2 : 2], identity[:])
             for part in parts:
                 nc.scalar.copy(v_bf[h][:, part, :].bitcast(F32), v_turned[:, :, part].rearrange("p u e -> p e u"))
 
@@ -169,11 +165,9 @@ def tile_attend_soft_topk_kernel(tc, qT, k_words, k_scales, vT, vs, offs, out):
         whole, halved = [slice(0, P)], [slice(0, P // 2), slice(P // 2, P)]
         for t in range(PACK):
             nc.tensor.transpose(probs_turned[:, t, :], probs[:, t, :], identity[:])
-        nc.scalar.activation(vs_slot[:], vs_turned[:, :, VS_ROW], ACT.Copy)
-        nc.scalar.activation(total[:], half_total[:, 0:1], ACT.Identity, bias=half_total[:, 1:2])
         turn_values(0, whole)
 
-        w_bf = late.tile([P, NQ, PACK], BF16, name="w_bf", align_bytes=64, offset=V1_AT + 2048)
+        w_bf = placed.tile([P, NQ, PACK], BF16, name="w_bf", align_bytes=64, offset=V1_AT + 2048)
         w_codes = sb.tile([P, NQ], U32, name="w_codes", align_bytes=64)
         w_scales = sb.tile([P, NQ], U8, name="w_scales", align_bytes=64)
         nc.vector.tensor_tensor(

@@ -1,7 +1,6 @@
 from contextlib import ExitStack
 
 import concourse.mybir as mybir
-from concourse.masks import make_identity
 
 F32 = mybir.dt.float32
 BF16 = mybir.dt.bfloat16
@@ -24,7 +23,7 @@ BANK = 2048
 VS_ROW = P - 1
 SCALES_FROM = 96
 V_AHEAD = 3 * T // 8
-ON_VECTOR = 288
+ON_VECTOR = 256
 
 FLOPS = 2 * NQ * N * (D + DV)
 
@@ -37,21 +36,25 @@ def tile_attend_soft_topk_kernel(tc, qT, k_words, k_scales, vT, vs, offs, out):
         ps = ctx.enter_context(tc.psum_pool(name="ps", bufs=1))
         banks = ctx.enter_context(tc.psum_pool(name="banks", bufs=1))
 
-        V0_AT, V1_AT, Q0_AT, Q1_AT, QC1_AT = 0, 8192, 16384, 18432, 20480
+        V0_AT, V1_AT, Q0_AT, Q1_AT, QC1_AT, VS_LISTED_AT, VS_AT = 0, 8192, 16384, 18432, 20480, 22528, 24576
 
         offsets = sb.tile([P, N // 16], U16, name="offsets")
         key_pool = sb.tile([P, T], I32, name="key_pool", align_bytes=64)
         key_scales = sb.tile([P, PASSES, N], U8, name="key_scales", align_bytes=64)
         identity = sb.tile([P, P], F32, name="identity", align_bytes=64)
         scale_pool = placed.tile([P, T], U8, name="scale_pool", align_bytes=64, offset=V1_AT)
-        vs_pool = sb.tile([P, T], F32, name="vs_pool", align_bytes=64)
+        vs_pool = placed.tile([P, T], F32, name="vs_pool", align_bytes=64, offset=VS_AT)
         q_raw = [placed.tile([P, PACK, NQ], F32, name=f"q_raw{o}", align_bytes=64, offset=at) for o, at in enumerate((Q0_AT, Q1_AT))]
         v_pools = [placed.tile([P, T], F32, name=f"v_pool{h}", align_bytes=64, offset=at) for h, at in enumerate((V0_AT, V1_AT))]
 
         nc.vector.memset(scale_pool[0:SCALES_FROM, :].bitcast(I32), 0)
         nc.vector.memset(key_scales[:].rearrange("p o i -> p (o i)").bitcast(I32), 0)
         nc.vector.memset(vs_pool[0:VS_ROW, :].bitcast(I32), 0)
-        make_identity(nc, identity[:])
+        off_diagonal = sb.tile([P, P], F32, name="off_diagonal", align_bytes=64)
+        distance = placed.tile([P, P], F32, name="distance", align_bytes=64, offset=VS_LISTED_AT)
+        nc.gpsimd.iota(off_diagonal[:], [[1, P]], base=0, channel_multiplier=-1, allow_small_or_imprecise_dtypes=True)
+        nc.scalar.activation(distance[:], off_diagonal[:], ACT.Abs)
+        nc.scalar.activation(identity[:], distance[:], ACT.Relu, bias=1.0, scale=-1.0)
 
         q_rows = qT[0].rearrange("(o p j) q -> o p j q", o=PASSES, j=PACK)
         nc.sync.dma_start(scale_pool[SCALES_FROM:P, :].bitcast(I32), k_scales.bitcast(I32).rearrange("o f t -> f o t"))
@@ -70,14 +73,14 @@ def tile_attend_soft_topk_kernel(tc, qT, k_words, k_scales, vT, vs, offs, out):
         nc.sync.dma_start(v_pools[0][:, V_AHEAD:T], vT[0:P, V_AHEAD:T])
         nc.sync.dma_start(v_pools[1][:], vT[P:DV, :])
 
-        vs_listed = sb.tile([P, N], F32, name="vs_listed", align_bytes=64)
+        vs_listed = placed.tile([P, N], F32, name="vs_listed", align_bytes=64, offset=VS_LISTED_AT)
         vs_turned = banks.tile([P, PACK, P], F32, name="vs_turned", offset=BANK)
         vs_slot = sb.tile([P, PACK], F32, name="vs_slot", align_bytes=64)
         nc.scalar.activation(vs_listed[:], vs_pool[:].indirect(offsets[:]), ACT.Copy)
         for t in range(PACK):
             nc.tensor.transpose(vs_turned[:, t, :], vs_listed[:, t:N:PACK], identity[:])
 
-        q_bf = [sb.tile([P, NQ, PACK], BF16, name=f"q_bf{o}", align_bytes=64) for o in range(PASSES)]
+        q_bf = [placed.tile([P, NQ, PACK], BF16, name=f"q_bf{o}", align_bytes=64, offset=VS_AT + 1024 * o) for o in range(PASSES)]
         q_codes = [
             sb.tile([P, NQ], U32, name="q_codes0", align_bytes=64),
             placed.tile([P, NQ], U32, name="q_codes1", align_bytes=64, offset=QC1_AT),

@@ -36,7 +36,7 @@ def tile_attend_soft_topk_kernel(tc, qT, k_words, k_scales, vT, vs, offs, out):
         ps = ctx.enter_context(tc.psum_pool(name="ps", bufs=1))
         banks = ctx.enter_context(tc.psum_pool(name="banks", bufs=1))
 
-        V0_AT, V1_AT, Q0_AT, Q1_AT, QC1_AT, VS_LISTED_AT, VS_AT = 0, 8192, 16384, 18432, 20480, 22528, 24576
+        V0_AT, V1_AT, Q0_AT, Q1_AT, QC1_AT, VS_LISTED_AT, VS_AT, MAX_AT = 0, 8192, 16384, 18432, 20480, 22528, 24576, 32768
 
         offsets = sb.tile([P, N // 16], U16, name="offsets")
         key_pool = sb.tile([P, T], I32, name="key_pool", align_bytes=64)
@@ -47,19 +47,19 @@ def tile_attend_soft_topk_kernel(tc, qT, k_words, k_scales, vT, vs, offs, out):
         q_raw = [placed.tile([P, PACK, NQ], F32, name=f"q_raw{o}", align_bytes=64, offset=at) for o, at in enumerate((Q0_AT, Q1_AT))]
         v_pools = [placed.tile([P, T], F32, name=f"v_pool{h}", align_bytes=64, offset=at) for h, at in enumerate((V0_AT, V1_AT))]
 
+        nc.scalar.dma_start(vs_pool[VS_ROW : VS_ROW + 1, :], vs[0:1, :])
         nc.vector.memset(scale_pool[0:SCALES_FROM, :].bitcast(I32), 0)
         nc.vector.memset(key_scales[:].rearrange("p o i -> p (o i)").bitcast(I32), 0)
-        nc.vector.memset(vs_pool[0:VS_ROW, :].bitcast(I32), 0)
         off_diagonal = sb.tile([P, P], F32, name="off_diagonal", align_bytes=64)
         distance = placed.tile([P, P], F32, name="distance", align_bytes=64, offset=VS_LISTED_AT)
         nc.gpsimd.iota(off_diagonal[:], [[1, P]], base=0, channel_multiplier=-1, allow_small_or_imprecise_dtypes=True)
+        nc.gpsimd.memset(vs_pool[0:VS_ROW, :].bitcast(I32), 0)
         nc.scalar.activation(distance[:], off_diagonal[:], ACT.Abs)
         nc.scalar.activation(identity[:], distance[:], ACT.Relu, bias=1.0, scale=-1.0)
 
         q_rows = qT[0].rearrange("(o p j) q -> o p j q", o=PASSES, j=PACK)
         nc.sync.dma_start(scale_pool[SCALES_FROM:P, :].bitcast(I32), k_scales.bitcast(I32).rearrange("o f t -> f o t"))
         nc.sync.dma_start(offsets[:], offs)
-        nc.sync.dma_start(vs_pool[VS_ROW : VS_ROW + 1, :], vs[0:1, :])
         nc.sync.dma_start(key_pool[:], k_words[0].rearrange("p t b -> p (t b)").bitcast(I32))
         for o in range(PASSES):
             nc.sync.dma_start(q_raw[o][:], q_rows[o])
@@ -118,13 +118,13 @@ def tile_attend_soft_topk_kernel(tc, qT, k_words, k_scales, vT, vs, offs, out):
                 stop=(o == PASSES - 1),
             )
 
-        neg_max = sb.tile([P, 1], F32, name="neg_max", align_bytes=64)
+        neg_max = placed.tile([P, 1], F32, name="neg_max", align_bytes=64, offset=MAX_AT)
         half_total = sb.tile([P, 2], F32, name="half_total")
         total = sb.tile([P, 1], F32, name="total")
         probs = sb.tile([P, PACK, P], F32, name="probs", align_bytes=64)
         v_listed = [
             placed.tile([P, N], BF16, name="v_listed0", align_bytes=64, offset=QC1_AT),
-            sb.tile([P, N], BF16, name="v_listed1", align_bytes=64),
+            placed.tile([P, N], BF16, name="v_listed1", align_bytes=64, offset=MAX_AT),
         ]
         nc.vector.tensor_reduce(neg_max[:], scores[:], AXIS.X, ALU.max, negate=True)
         nc.vector.tensor_copy(v_listed[0][:], v_pools[0][:].indirect(offsets[:]))

@@ -22,7 +22,7 @@ V_BLOCKS = DV // P
 BANK = 2048
 VS_ROW = P - 1
 SCALES_FROM = 96
-V_AHEAD = 3 * T // 8
+V_AHEAD = 7 * T // 16
 ON_VECTOR = 256
 
 FLOPS = 2 * NQ * N * (D + DV)

@@ -24,6 +24,7 @@ VS_ROW = P - 1
 SCALES_FROM = 96
 V_AHEAD = 7 * T // 16
 ON_VECTOR = 256
+RUN = 16
 
 FLOPS = 2 * NQ * N * (D + DV)
 
@@ -39,19 +40,19 @@ def tile_attend_soft_topk_kernel(tc, qT, k_words, k_scales, vT, vs, offs, out):
         V0_AT, V1_AT, Q0_AT, Q1_AT, QC1_AT, VS_LISTED_AT, VS_AT, MAX_AT = 0, 8192, 16384, 18432, 20480, 22528, 24576, 32768
 
         offsets = sb.tile([P, N // 16], U16, name="offsets")
-        key_pool = sb.tile([P, T], I32, name="key_pool", align_bytes=64)
-        key_scales = sb.tile([P, PASSES, N], U8, name="key_scales", align_bytes=64)
-        identity = sb.tile([P, P], F32, name="identity", align_bytes=64)
-        scale_pool = placed.tile([P, T], U8, name="scale_pool", align_bytes=64, offset=V1_AT)
-        vs_pool = placed.tile([P, T], F32, name="vs_pool", align_bytes=64, offset=VS_AT)
-        q_raw = [placed.tile([P, PACK, NQ], F32, name=f"q_raw{o}", align_bytes=64, offset=at) for o, at in enumerate((Q0_AT, Q1_AT))]
-        v_pools = [placed.tile([P, T], F32, name=f"v_pool{h}", align_bytes=64, offset=at) for h, at in enumerate((V0_AT, V1_AT))]
+        key_pool = sb.tile([P, T], I32, name="key_pool", align_bytes=256)
+        key_scales = sb.tile([P, PASSES, N], U8, name="key_scales", align_bytes=256)
+        identity = sb.tile([P, P], F32, name="identity", align_bytes=256)
+        scale_pool = placed.tile([P, T], U8, name="scale_pool", align_bytes=256, offset=V1_AT)
+        vs_pool = placed.tile([P, T], F32, name="vs_pool", align_bytes=256, offset=VS_AT)
+        q_raw = [placed.tile([P, PACK, NQ], F32, name=f"q_raw{o}", align_bytes=256, offset=at) for o, at in enumerate((Q0_AT, Q1_AT))]
+        v_pools = [placed.tile([P, T], F32, name=f"v_pool{h}", align_bytes=256, offset=at) for h, at in enumerate((V0_AT, V1_AT))]
 
         nc.scalar.dma_start(vs_pool[VS_ROW : VS_ROW + 1, :], vs[0:1, :])
         nc.vector.memset(scale_pool[0:SCALES_FROM, :].bitcast(I32), 0)
         nc.vector.memset(key_scales[:].rearrange("p o i -> p (o i)").bitcast(I32), 0)
-        off_diagonal = sb.tile([P, P], F32, name="off_diagonal", align_bytes=64)
-        distance = placed.tile([P, P], F32, name="distance", align_bytes=64, offset=VS_LISTED_AT)
+        off_diagonal = sb.tile([P, P], F32, name="off_diagonal", align_bytes=256)
+        distance = placed.tile([P, P], F32, name="distance", align_bytes=256, offset=VS_LISTED_AT)
         nc.gpsimd.iota(off_diagonal[:], [[1, P]], base=0, channel_multiplier=-1, allow_small_or_imprecise_dtypes=True)
         nc.gpsimd.memset(vs_pool[0:VS_ROW, :].bitcast(I32), 0)
         nc.scalar.activation(distance[:], off_diagonal[:], ACT.Abs)
@@ -65,7 +66,7 @@ def tile_attend_soft_topk_kernel(tc, qT, k_words, k_scales, vT, vs, offs, out):
             nc.sync.dma_start(q_raw[o][:], q_rows[o])
         nc.sync.dma_start(v_pools[0][:, 0:V_AHEAD], vT[0:P, 0:V_AHEAD])
 
-        listed_scales = sb.tile([P, N], U8, name="listed_scales", align_bytes=64)
+        listed_scales = sb.tile([P, N], U8, name="listed_scales", align_bytes=256)
         nc.vector.tensor_copy(listed_scales[:], scale_pool[:].indirect(offsets[:]))
         for a in range(4):
             rows = slice(SCALES_FROM + 8 * a, SCALES_FROM + 8 * a + 8)
@@ -73,19 +74,21 @@ def tile_attend_soft_topk_kernel(tc, qT, k_words, k_scales, vT, vs, offs, out):
         nc.sync.dma_start(v_pools[0][:, V_AHEAD:T], vT[0:P, V_AHEAD:T])
         nc.sync.dma_start(v_pools[1][:], vT[P:DV, :])
 
-        vs_listed = placed.tile([P, N], F32, name="vs_listed", align_bytes=64, offset=VS_LISTED_AT)
+        vs_listed = placed.tile([P, N], F32, name="vs_listed", align_bytes=256, offset=VS_LISTED_AT)
         vs_turned = banks.tile([P, PACK, P], F32, name="vs_turned", offset=BANK)
-        vs_slot = sb.tile([P, PACK], F32, name="vs_slot", align_bytes=64)
+        vs_slot = sb.tile([P, PACK], F32, name="vs_slot", align_bytes=256)
         nc.scalar.activation(vs_listed[:], vs_pool[:].indirect(offsets[:]), ACT.Copy)
+        vs_dealt = sb.tile([P, 2, N // 2], F32, name="vs_dealt", align_bytes=256)
+        nc.scalar.copy(vs_dealt[:].rearrange("p u (b s) -> p u b s", s=RUN), vs_listed[:].rearrange("p (b u s) -> p u b s", u=2, s=RUN))
         for t in range(PACK):
-            nc.tensor.transpose(vs_turned[:, t, :], vs_listed[:, t:N:PACK], identity[:])
+            nc.tensor.transpose(vs_turned[:, t, :], vs_dealt[:, t // 2, t % 2 : N // 2 : 2], identity[:])
 
-        q_bf = [placed.tile([P, NQ, PACK], BF16, name=f"q_bf{o}", align_bytes=64, offset=VS_AT + 1024 * o) for o in range(PASSES)]
+        q_bf = [placed.tile([P, NQ, PACK], BF16, name=f"q_bf{o}", align_bytes=256, offset=VS_AT + 1024 * o) for o in range(PASSES)]
         q_codes = [
-            sb.tile([P, NQ], U32, name="q_codes0", align_bytes=64),
-            placed.tile([P, NQ], U32, name="q_codes1", align_bytes=64, offset=QC1_AT),
+            sb.tile([P, NQ], U32, name="q_codes0", align_bytes=256),
+            placed.tile([P, NQ], U32, name="q_codes1", align_bytes=256, offset=QC1_AT),
         ]
-        q_scales = [sb.tile([P, NQ], U8, name=f"q_scales{o}", align_bytes=64) for o in range(PASSES)]
+        q_scales = [sb.tile([P, NQ], U8, name=f"q_scales{o}", align_bytes=256) for o in range(PASSES)]
         for o in range(PASSES):
             nc.scalar.activation(
                 q_bf[o][:].rearrange("p (c i) j -> p c j i", i=4),
@@ -97,8 +100,8 @@ def tile_attend_soft_topk_kernel(tc, qT, k_words, k_scales, vT, vs, offs, out):
         def quantise_queries(o):
             nc.vector.quantize_mx(q_codes[o][:].bitcast(FP8X4), q_scales[o][:], q_bf[o][:].rearrange("p q j -> p (q j)"))
 
-        key_pairs = sb.tile([P, N], U32, name="key_pairs", align_bytes=64)
-        key_words = [placed.tile([P, 2 * N], U8, name=f"key_words{o}", align_bytes=64, offset=at) for o, at in enumerate((Q0_AT, Q1_AT))]
+        key_pairs = sb.tile([P, N], U32, name="key_pairs", align_bytes=256)
+        key_words = [placed.tile([P, 2 * N], U8, name=f"key_words{o}", align_bytes=256, offset=at) for o, at in enumerate((Q0_AT, Q1_AT))]
         nc.vector.tensor_copy(key_pairs[:], key_pool[:].bitcast(U32).indirect(offsets[:]))
         halves = key_pairs[:].bitcast(U16).rearrange("p (i o) -> p o i", o=PASSES)
         quantise_queries(0)
@@ -118,44 +121,49 @@ def tile_attend_soft_topk_kernel(tc, qT, k_words, k_scales, vT, vs, offs, out):
                 stop=(o == PASSES - 1),
             )
 
-        neg_max = placed.tile([P, 1], F32, name="neg_max", align_bytes=64, offset=MAX_AT)
+        neg_max = placed.tile([P, 1], F32, name="neg_max", align_bytes=256, offset=MAX_AT)
         half_total = sb.tile([P, 2], F32, name="half_total")
         total = sb.tile([P, 1], F32, name="total")
-        probs = sb.tile([P, PACK, P], F32, name="probs", align_bytes=64)
+        probs = sb.tile([P, PACK, P], F32, name="probs", align_bytes=256)
         v_listed = [
-            placed.tile([P, N], BF16, name="v_listed0", align_bytes=64, offset=QC1_AT),
-            placed.tile([P, N], BF16, name="v_listed1", align_bytes=64, offset=MAX_AT),
+            placed.tile([P, N], BF16, name="v_listed0", align_bytes=256, offset=QC1_AT),
+            placed.tile([P, N], BF16, name="v_listed1", align_bytes=256, offset=MAX_AT),
         ]
         nc.vector.tensor_reduce(neg_max[:], scores[:], AXIS.X, ALU.max, negate=True)
-        nc.vector.tensor_copy(v_listed[0][:], v_pools[0][:].indirect(offsets[:]))
-        score_planes = scores[:].rearrange("q (s t) -> q t s", t=PACK)
+        v_dealt = [tile[:].rearrange("p (u b s) -> p b u s", u=2, s=RUN) for tile in v_listed]
+        nc.vector.tensor_copy(v_dealt[0], v_pools[0][:].indirect(offsets[:]))
+        score_planes = scores[:].rearrange("q (b u j e) -> q u e b j", u=2, j=RUN // 2, e=2)
         probs_turned = ps.tile([P, PACK, NQ], F32, name="probs_turned")
         for half in range(2):
             planes = slice(2 * half, 2 * half + 2)
             nc.scalar.activation(
-                probs[:, planes, :], score_planes[:, planes, :], ACT.Exp, bias=neg_max[:], accum_out=half_total[:, half : half + 1]
+                probs[:, planes, :].rearrange("q e (b j) -> q e b j", j=RUN // 2),
+                score_planes[:, half],
+                ACT.Exp,
+                bias=neg_max[:],
+                accum_out=half_total[:, half : half + 1],
             )
         nc.scalar.activation(total[:], half_total[:, 0:1], ACT.Identity, bias=half_total[:, 1:2])
         cut = ON_VECTOR // 16
-        nc.vector.tensor_copy(v_listed[1][:, 0:ON_VECTOR], v_pools[1][:].indirect(offsets[:, 0:cut]))
-        nc.scalar.activation(v_listed[1][:, ON_VECTOR:N], v_pools[1][:].indirect(offsets[:, cut : N // 16]), ACT.Copy)
+        nc.vector.tensor_copy(v_dealt[1][:, 0 : cut // 2], v_pools[1][:].indirect(offsets[:, 0:cut]))
+        nc.scalar.activation(v_dealt[1][:, cut // 2 : N // 32], v_pools[1][:].indirect(offsets[:, cut : N // 16]), ACT.Copy)
 
         v_codes = [
-            placed.tile([P, P], U32, name="v_codes0", align_bytes=64, offset=V1_AT + 512),
-            sb.tile([P, P], U32, name="v_codes1", align_bytes=64),
+            placed.tile([P, P], U32, name="v_codes0", align_bytes=256, offset=V1_AT + 512),
+            sb.tile([P, P], U32, name="v_codes1", align_bytes=256),
         ]
-        inv_total = placed.tile([P, 1], F32, name="inv_total", align_bytes=64, offset=V1_AT + 1024)
-        v_scales = [sb.tile([P, P], U8, name=f"v_scales{h}", align_bytes=64) for h in range(V_BLOCKS)]
+        inv_total = placed.tile([P, 1], F32, name="inv_total", align_bytes=256, offset=V1_AT + 1024)
+        v_scales = [sb.tile([P, P], U8, name=f"v_scales{h}", align_bytes=256) for h in range(V_BLOCKS)]
         v_bf = [
-            placed.tile([P, P, PACK], BF16, name="v_bf0", align_bytes=64, offset=V1_AT + 4096),
-            sb.tile([P, P, PACK], BF16, name="v_bf1", align_bytes=64),
+            placed.tile([P, P, PACK], BF16, name="v_bf0", align_bytes=256, offset=V1_AT + 4096),
+            sb.tile([P, P, PACK], BF16, name="v_bf1", align_bytes=256),
         ]
 
         def turn_values(h, parts):
             v_turned = banks.tile([P, 2, P], F32, name=f"v_turned{h}", offset=BANK * h)
             words = v_listed[h][:].bitcast(F32)
             for u in range(2):
-                nc.tensor.transpose(v_turned[:, u, :], words[:, u : N // 2 : 2], identity[:])
+                nc.tensor.transpose(v_turned[:, u, :], words[:, u * P : (u + 1) * P], identity[:])
             for part in parts:
                 nc.scalar.copy(v_bf[h][:, part, :].bitcast(F32), v_turned[:, :, part].rearrange("p u e -> p e u"))
 
@@ -170,9 +178,9 @@ def tile_attend_soft_topk_kernel(tc, qT, k_words, k_scales, vT, vs, offs, out):
             nc.tensor.transpose(probs_turned[:, t, :], probs[:, t, :], identity[:])
         turn_values(0, whole)
 
-        w_bf = placed.tile([P, NQ, PACK], BF16, name="w_bf", align_bytes=64, offset=V1_AT + 2048)
-        w_codes = sb.tile([P, NQ], U32, name="w_codes", align_bytes=64)
-        w_scales = sb.tile([P, NQ], U8, name="w_scales", align_bytes=64)
+        w_bf = placed.tile([P, NQ, PACK], BF16, name="w_bf", align_bytes=256, offset=V1_AT + 2048)
+        w_codes = sb.tile([P, NQ], U32, name="w_codes", align_bytes=256)
+        w_scales = sb.tile([P, NQ], U8, name="w_scales", align_bytes=256)
         nc.vector.tensor_tensor(
             w_bf[:],
             probs_turned[:].rearrange("p t q -> p q t"),
@@ -188,7 +196,7 @@ def tile_attend_soft_topk_kernel(tc, qT, k_words, k_scales, vT, vs, offs, out):
         for h in range(V_BLOCKS):
             cols = slice(h * P, (h + 1) * P)
             sums = ps.tile([P, P], F32, name=f"sums{h}")
-            result = sb.tile([P, P], F32, name=f"result{h}")
+            result = sb.tile([P, P], F32, name=f"result{h}", align_bytes=256)
             nc.tensor.matmul_mx(
                 sums[:],
                 lhsT=w_codes[:].bitcast(FP8X4),

@@ -37,7 +37,7 @@ def tile_attend_soft_topk_kernel(tc, qT, k_words, k_scales, vT, vs, offs, out):
         ps = ctx.enter_context(tc.psum_pool(name="ps", bufs=1))
         banks = ctx.enter_context(tc.psum_pool(name="banks", bufs=1))
 
-        V0_AT, V1_AT, Q0_AT, Q1_AT, QC1_AT, VS_LISTED_AT, VS_AT, MAX_AT = 0, 8192, 16384, 18432, 20480, 22528, 24576, 32768
+        V0_AT, V1_AT, Q0_AT, Q1_AT, QC1_AT, VS_LISTED_AT, VS_AT, MAX_AT, VS_SLOT_AT = 0, 8192, 16384, 18432, 20480, 22528, 24576, 32768, 33792
 
         offsets = sb.tile([P, N // 16], U16, name="offsets")
         key_pool = sb.tile([P, T], I32, name="key_pool", align_bytes=256)
@@ -76,7 +76,7 @@ def tile_attend_soft_topk_kernel(tc, qT, k_words, k_scales, vT, vs, offs, out):
 
         vs_listed = placed.tile([P, N], F32, name="vs_listed", align_bytes=256, offset=VS_LISTED_AT)
         vs_turned = banks.tile([P, PACK, P], F32, name="vs_turned", offset=BANK)
-        vs_slot = sb.tile([P, PACK], F32, name="vs_slot", align_bytes=256)
+        vs_slot = placed.tile([P, PACK], F32, name="vs_slot", align_bytes=256, offset=VS_SLOT_AT)
         nc.scalar.activation(vs_listed[:], vs_pool[:].indirect(offsets[:]), ACT.Copy)
         vs_dealt = sb.tile([P, 2, N // 2], F32, name="vs_dealt", align_bytes=256)
         nc.scalar.copy(vs_dealt[:].rearrange("p u (b s) -> p u b s", s=RUN), vs_listed[:].rearrange("p (b u s) -> p u b s", u=2, s=RUN))
@@ -131,7 +131,13 @@ def tile_attend_soft_topk_kernel(tc, qT, k_words, k_scales, vT, vs, offs, out):
         ]
         nc.vector.tensor_reduce(neg_max[:], scores[:], AXIS.X, ALU.max, negate=True)
         v_dealt = [tile[:].rearrange("p (u b s) -> p b u s", u=2, s=RUN) for tile in v_listed]
-        nc.vector.tensor_copy(v_dealt[0], v_pools[0][:].indirect(offsets[:]))
+        cut = ON_VECTOR // 16
+
+        def gather_values(h):
+            nc.vector.tensor_copy(v_dealt[h][:, 0 : cut // 2], v_pools[h][:].indirect(offsets[:, 0:cut]))
+            nc.scalar.activation(v_dealt[h][:, cut // 2 : N // 32], v_pools[h][:].indirect(offsets[:, cut : N // 16]), ACT.Copy)
+
+        gather_values(0)
         score_planes = scores[:].rearrange("q (b u j e) -> q u e b j", u=2, j=RUN // 2, e=2)
         probs_turned = ps.tile([P, PACK, NQ], F32, name="probs_turned")
         for half in range(2):
@@ -144,20 +150,12 @@ def tile_attend_soft_topk_kernel(tc, qT, k_words, k_scales, vT, vs, offs, out):
                 accum_out=half_total[:, half : half + 1],
             )
         nc.scalar.activation(total[:], half_total[:, 0:1], ACT.Identity, bias=half_total[:, 1:2])
-        cut = ON_VECTOR // 16
-        nc.vector.tensor_copy(v_dealt[1][:, 0 : cut // 2], v_pools[1][:].indirect(offsets[:, 0:cut]))
-        nc.scalar.activation(v_dealt[1][:, cut // 2 : N // 32], v_pools[1][:].indirect(offsets[:, cut : N // 16]), ACT.Copy)
+        gather_values(1)
 
-        v_codes = [
-            placed.tile([P, P], U32, name="v_codes0", align_bytes=256, offset=V1_AT + 512),
-            sb.tile([P, P], U32, name="v_codes1", align_bytes=256),
-        ]
-        inv_total = placed.tile([P, 1], F32, name="inv_total", align_bytes=256, offset=V1_AT + 1024)
+        v_codes = [sb.tile([P, P], U32, name=f"v_codes{h}", align_bytes=256) for h in range(V_BLOCKS)]
+        inv_total = placed.tile([P, 1], F32, name="inv_total", align_bytes=256, offset=VS_SLOT_AT)
         v_scales = [sb.tile([P, P], U8, name=f"v_scales{h}", align_bytes=256) for h in range(V_BLOCKS)]
-        v_bf = [
-            placed.tile([P, P, PACK], BF16, name="v_bf0", align_bytes=256, offset=V1_AT + 4096),
-            sb.tile([P, P, PACK], BF16, name="v_bf1", align_bytes=256),
-        ]
+        v_bf = [sb.tile([P, P, PACK], BF16, name=f"v_bf{h}", align_bytes=256) for h in range(V_BLOCKS)]
 
         def turn_values(h, parts):
             v_turned = banks.tile([P, 2, P], F32, name=f"v_turned{h}", offset=BANK * h)
@@ -178,7 +176,7 @@ def tile_attend_soft_topk_kernel(tc, qT, k_words, k_scales, vT, vs, offs, out):
             nc.tensor.transpose(probs_turned[:, t, :], probs[:, t, :], identity[:])
         turn_values(0, whole)
 
-        w_bf = placed.tile([P, NQ, PACK], BF16, name="w_bf", align_bytes=256, offset=V1_AT + 2048)
+        w_bf = sb.tile([P, NQ, PACK], BF16, name="w_bf", align_bytes=256)
         w_codes = sb.tile([P, NQ], U32, name="w_codes", align_bytes=256)
         w_scales = sb.tile([P, NQ], U8, name="w_scales", align_bytes=256)
         nc.vector.tensor_tensor(
@@ -189,8 +187,8 @@ def tile_attend_soft_topk_kernel(tc, qT, k_words, k_scales, vT, vs, offs, out):
         )
         turn_values(1, halved)
         quantise_values(0, whole)
-        nc.vector.reciprocal(inv_total[:], total[:])
         nc.vector.quantize_mx(w_codes[:].bitcast(FP8X4), w_scales[:], w_bf[:].rearrange("p q t -> p (q t)"))
+        nc.vector.reciprocal(inv_total[:], total[:])
         quantise_values(1, halved)
 
         for h in range(V_BLOCKS):

@@ -122,7 +122,7 @@ def tile_attend_soft_topk_kernel(tc, qT, k_words, k_scales, vT, vs, offs, out):
             )
 
         neg_max = placed.tile([P, 1], F32, name="neg_max", align_bytes=256, offset=MAX_AT)
-        half_total = sb.tile([P, 2], F32, name="half_total")
+        part_total = sb.tile([P, 3], F32, name="part_total")
         total = sb.tile([P, 1], F32, name="total")
         probs = sb.tile([P, PACK, P], F32, name="probs", align_bytes=256)
         v_listed = [
@@ -138,18 +138,14 @@ def tile_attend_soft_topk_kernel(tc, qT, k_words, k_scales, vT, vs, offs, out):
             nc.scalar.activation(v_dealt[h][:, cut // 2 : N // 32], v_pools[h][:].indirect(offsets[:, cut : N // 16]), ACT.Copy)
 
         gather_values(0)
-        score_planes = scores[:].rearrange("q (b u j e) -> q u e b j", u=2, j=RUN // 2, e=2)
         probs_turned = ps.tile([P, PACK, NQ], F32, name="probs_turned")
-        for half in range(2):
-            planes = slice(2 * half, 2 * half + 2)
+        score_planes = scores[:].rearrange("q (b u j e) -> q u e b j", u=2, j=RUN // 2, e=2)
+        prob_planes = probs[:].rearrange("q (u e) (b j) -> q u e b j", u=2, j=RUN // 2)
+        for piece, (u, places) in enumerate(((0, slice(0, 2)), (1, slice(0, 1)), (1, slice(1, 2)))):
             nc.scalar.activation(
-                probs[:, planes, :].rearrange("q e (b j) -> q e b j", j=RUN // 2),
-                score_planes[:, half],
-                ACT.Exp,
-                bias=neg_max[:],
-                accum_out=half_total[:, half : half + 1],
+                prob_planes[:, u, places], score_planes[:, u, places], ACT.Exp, bias=neg_max[:], accum_out=part_total[:, piece : piece + 1]
             )
-        nc.scalar.activation(total[:], half_total[:, 0:1], ACT.Identity, bias=half_total[:, 1:2])
+        nc.vector.tensor_reduce(total[:], part_total[:], AXIS.X, ALU.add)
         gather_values(1)
 
         v_codes = [sb.tile([P, P], U32, name=f"v_codes{h}", align_bytes=256) for h in range(V_BLOCKS)]

@@ -141,7 +141,7 @@ def tile_attend_soft_topk_kernel(tc, qT, k_words, k_scales, vT, vs, offs, out):
         probs_turned = ps.tile([P, PACK, NQ], F32, name="probs_turned")
         score_planes = scores[:].rearrange("q (b u j e) -> q u e b j", u=2, j=RUN // 2, e=2)
         prob_planes = probs[:].rearrange("q (u e) (b j) -> q u e b j", u=2, j=RUN // 2)
-        for piece, (u, places) in enumerate(((0, slice(0, 2)), (1, slice(0, 1)), (1, slice(1, 2)))):
+        for piece, (u, places) in enumerate(((0, slice(0, 1)), (0, slice(1, 2)), (1, slice(0, 2)))):
             nc.scalar.activation(
                 prob_planes[:, u, places], score_planes[:, u, places], ACT.Exp, bias=neg_max[:], accum_out=part_total[:, piece : piece + 1]
             )
@@ -187,21 +187,21 @@ def tile_attend_soft_topk_kernel(tc, qT, k_words, k_scales, vT, vs, offs, out):
         nc.vector.reciprocal(inv_total[:], total[:])
         quantise_values(1, halved)
 
-        for h in range(V_BLOCKS):
-            cols = slice(h * P, (h + 1) * P)
-            sums = ps.tile([P, P], F32, name=f"sums{h}")
+        for h, parts in enumerate((whole, halved)):
             result = sb.tile([P, P], F32, name=f"result{h}", align_bytes=256)
-            nc.tensor.matmul_mx(
-                sums[:],
-                lhsT=w_codes[:].bitcast(FP8X4),
-                lhsT_scale=w_scales[:],
-                rhs=v_codes[h][:].bitcast(FP8X4),
-                rhs_scale=v_scales[h][:],
-                start=True,
-                stop=True,
-            )
-            if h == 1:
-                nc.vector.tensor_scalar(result[:], sums[:], inv_total[:], None, ALU.mult)
-            else:
-                nc.scalar.activation(result[:], sums[:], ACT.Copy, scale=inv_total[:])
-            nc.sync.dma_start(out[0][:, cols], result[:])
+            for part in parts:
+                sums = ps.tile([P, part.stop - part.start], F32, name=f"sums{h}_{part.start}")
+                nc.tensor.matmul_mx(
+                    sums[:],
+                    lhsT=w_codes[:].bitcast(FP8X4),
+                    lhsT_scale=w_scales[:],
+                    rhs=v_codes[h][:, part].bitcast(FP8X4),
+                    rhs_scale=v_scales[h][:, part],
+                    start=True,
+                    stop=True,
+                )
+                if h == 1 and part.stop == P:
+                    nc.vector.tensor_scalar(result[:, part], sums[:], inv_total[:], None, ALU.mult)
+                else:
+                    nc.scalar.activation(result[:, part], sums[:], ACT.Copy, scale=inv_total[:])
+            nc.sync.dma_start(out[0][:, h * P : (h + 1) * P], result[:])

@@ -23,7 +23,7 @@ BANK = 2048
 VS_ROW = P - 1
 SCALES_FROM = 96
 V_AHEAD = 7 * T // 16
-ON_VECTOR = 256
+ON_VECTOR = (288, 256)
 RUN = 16
 
 FLOPS = 2 * NQ * N * (D + DV)
@@ -37,22 +37,22 @@ def tile_attend_soft_topk_kernel(tc, qT, k_words, k_scales, vT, vs, offs, out):
         ps = ctx.enter_context(tc.psum_pool(name="ps", bufs=1))
         banks = ctx.enter_context(tc.psum_pool(name="banks", bufs=1))
 
-        V0_AT, V1_AT, Q0_AT, Q1_AT, QC1_AT, VS_LISTED_AT, VS_AT, MAX_AT, VS_SLOT_AT = 0, 8192, 16384, 18432, 20480, 22528, 24576, 32768, 33792
+        V0_AT, V1_AT, SCALES_AT, Q0_AT, Q1_AT, QC1_AT, VS_AT = 0, 8192, 15360, 17408, 19456, 21504, 24576
+        MAX_AT, VS_SLOT_AT = 32768, 33792
 
         offsets = sb.tile([P, N // 16], U16, name="offsets")
         key_pool = sb.tile([P, T], I32, name="key_pool", align_bytes=256)
-        key_scales = sb.tile([P, PASSES, N], U8, name="key_scales", align_bytes=256)
+        key_scales = placed.tile([P, PASSES, N], U8, name="key_scales", align_bytes=256, offset=SCALES_AT + T // 2)
         identity = sb.tile([P, P], F32, name="identity", align_bytes=256)
-        scale_pool = placed.tile([P, T], U8, name="scale_pool", align_bytes=256, offset=V1_AT)
+        scale_pool = placed.tile([P, T], U8, name="scale_pool", align_bytes=256, offset=SCALES_AT)
         vs_pool = placed.tile([P, T], F32, name="vs_pool", align_bytes=256, offset=VS_AT)
         q_raw = [placed.tile([P, PACK, NQ], F32, name=f"q_raw{o}", align_bytes=256, offset=at) for o, at in enumerate((Q0_AT, Q1_AT))]
         v_pools = [placed.tile([P, T], F32, name=f"v_pool{h}", align_bytes=256, offset=at) for h, at in enumerate((V0_AT, V1_AT))]
 
         nc.scalar.dma_start(vs_pool[VS_ROW : VS_ROW + 1, :], vs[0:1, :])
         nc.vector.memset(scale_pool[0:SCALES_FROM, :].bitcast(I32), 0)
-        nc.vector.memset(key_scales[:].rearrange("p o i -> p (o i)").bitcast(I32), 0)
         off_diagonal = sb.tile([P, P], F32, name="off_diagonal", align_bytes=256)
-        distance = placed.tile([P, P], F32, name="distance", align_bytes=256, offset=VS_LISTED_AT)
+        distance = sb.tile([P, P], F32, name="distance", align_bytes=256)
         nc.gpsimd.iota(off_diagonal[:], [[1, P]], base=0, channel_multiplier=-1, allow_small_or_imprecise_dtypes=True)
         nc.gpsimd.memset(vs_pool[0:VS_ROW, :].bitcast(I32), 0)
         nc.scalar.activation(distance[:], off_diagonal[:], ACT.Abs)
@@ -74,7 +74,7 @@ def tile_attend_soft_topk_kernel(tc, qT, k_words, k_scales, vT, vs, offs, out):
         nc.sync.dma_start(v_pools[0][:, V_AHEAD:T], vT[0:P, V_AHEAD:T])
         nc.sync.dma_start(v_pools[1][:], vT[P:DV, :])
 
-        vs_listed = placed.tile([P, N], F32, name="vs_listed", align_bytes=256, offset=VS_LISTED_AT)
+        vs_listed = sb.tile([P, N], F32, name="vs_listed", align_bytes=256)
         vs_turned = banks.tile([P, PACK, P], F32, name="vs_turned", offset=BANK)
         vs_slot = placed.tile([P, PACK], F32, name="vs_slot", align_bytes=256, offset=VS_SLOT_AT)
         nc.scalar.activation(vs_listed[:], vs_pool[:].indirect(offsets[:]), ACT.Copy)
@@ -122,7 +122,7 @@ def tile_attend_soft_topk_kernel(tc, qT, k_words, k_scales, vT, vs, offs, out):
             )
 
         neg_max = placed.tile([P, 1], F32, name="neg_max", align_bytes=256, offset=MAX_AT)
-        part_total = sb.tile([P, 3], F32, name="part_total")
+        part_total = sb.tile([P, PACK], F32, name="part_total")
         total = sb.tile([P, 1], F32, name="total")
         probs = sb.tile([P, PACK, P], F32, name="probs", align_bytes=256)
         v_listed = [
@@ -131,9 +131,9 @@ def tile_attend_soft_topk_kernel(tc, qT, k_words, k_scales, vT, vs, offs, out):
         ]
         nc.vector.tensor_reduce(neg_max[:], scores[:], AXIS.X, ALU.max, negate=True)
         v_dealt = [tile[:].rearrange("p (u b s) -> p b u s", u=2, s=RUN) for tile in v_listed]
-        cut = ON_VECTOR // 16
 
         def gather_values(h):
+            cut = ON_VECTOR[h] // 16
             nc.vector.tensor_copy(v_dealt[h][:, 0 : cut // 2], v_pools[h][:].indirect(offsets[:, 0:cut]))
             nc.scalar.activation(v_dealt[h][:, cut // 2 : N // 32], v_pools[h][:].indirect(offsets[:, cut : N // 16]), ACT.Copy)
 
@@ -141,10 +141,9 @@ def tile_attend_soft_topk_kernel(tc, qT, k_words, k_scales, vT, vs, offs, out):
         probs_turned = ps.tile([P, PACK, NQ], F32, name="probs_turned")
         score_planes = scores[:].rearrange("q (b u j e) -> q u e b j", u=2, j=RUN // 2, e=2)
         prob_planes = probs[:].rearrange("q (u e) (b j) -> q u e b j", u=2, j=RUN // 2)
-        for piece, (u, places) in enumerate(((0, slice(0, 1)), (0, slice(1, 2)), (1, slice(0, 2)))):
-            nc.scalar.activation(
-                prob_planes[:, u, places], score_planes[:, u, places], ACT.Exp, bias=neg_max[:], accum_out=part_total[:, piece : piece + 1]
-            )
+        for t in range(PACK):
+            u, e = divmod(t, 2)
+            nc.scalar.activation(prob_planes[:, u, e], score_planes[:, u, e], ACT.Exp, bias=neg_max[:], accum_out=part_total[:, t : t + 1])
         nc.vector.tensor_reduce(total[:], part_total[:], AXIS.X, ALU.add)
         gather_values(1)
 

from contextlib import ExitStack

import concourse.mybir as mybir

F32 = mybir.dt.float32
BF16 = mybir.dt.bfloat16
I32 = mybir.dt.int32
U32 = mybir.dt.uint32
U16 = mybir.dt.uint16
U8 = mybir.dt.uint8
FP8X4 = mybir.dt.float8_e4m3fn_x4
FP4X4 = mybir.dt.float4_e2m1fn_x4
ACT = mybir.ActivationFunctionType
ALU = mybir.AluOpType
AXIS = mybir.AxisListType

P = 128
PACK = 4
N, T, D, DV, NQ = 512, 2048, 1024, 256, 128
PASSES = D // (P * PACK)
V_BLOCKS = DV // P
BANK = 2048
VS_ROW = P - 1
SCALES_FROM = 96
V_AHEAD = 7 * T // 16
ON_VECTOR = (288, 256)
RUN = 16

FLOPS = 2 * NQ * N * (D + DV)


def tile_attend_soft_topk_kernel(tc, qT, k_words, k_scales, vT, vs, offs, out):
    nc = tc.nc
    with ExitStack() as ctx:
        sb = ctx.enter_context(tc.tile_pool(name="sb", bufs=1))
        placed = ctx.enter_context(tc.tile_pool(name="placed", bufs=1))
        ps = ctx.enter_context(tc.psum_pool(name="ps", bufs=1))
        banks = ctx.enter_context(tc.psum_pool(name="banks", bufs=1))

        V0_AT, V1_AT, SCALES_AT, Q0_AT, Q1_AT, QC1_AT, VS_AT = 0, 8192, 15360, 17408, 19456, 21504, 24576
        MAX_AT, VS_SLOT_AT = 32768, 33792

        offsets = sb.tile([P, N // 16], U16, name="offsets")
        key_pool = sb.tile([P, T], I32, name="key_pool", align_bytes=256)
        key_scales = placed.tile([P, PASSES, N], U8, name="key_scales", align_bytes=256, offset=SCALES_AT + T // 2)
        identity = sb.tile([P, P], F32, name="identity", align_bytes=256)
        scale_pool = placed.tile([P, T], U8, name="scale_pool", align_bytes=256, offset=SCALES_AT)
        vs_pool = placed.tile([P, T], F32, name="vs_pool", align_bytes=256, offset=VS_AT)
        q_raw = [placed.tile([P, PACK, NQ], F32, name=f"q_raw{o}", align_bytes=256, offset=at) for o, at in enumerate((Q0_AT, Q1_AT))]
        v_pools = [placed.tile([P, T], F32, name=f"v_pool{h}", align_bytes=256, offset=at) for h, at in enumerate((V0_AT, V1_AT))]

        nc.scalar.dma_start(vs_pool[VS_ROW : VS_ROW + 1, :], vs[0:1, :])
        nc.vector.memset(scale_pool[0:SCALES_FROM, :].bitcast(I32), 0)
        off_diagonal = sb.tile([P, P], F32, name="off_diagonal", align_bytes=256)
        distance = sb.tile([P, P], F32, name="distance", align_bytes=256)
        nc.gpsimd.iota(off_diagonal[:], [[1, P]], base=0, channel_multiplier=-1, allow_small_or_imprecise_dtypes=True)
        nc.gpsimd.memset(vs_pool[0:VS_ROW, :].bitcast(I32), 0)
        nc.scalar.activation(distance[:], off_diagonal[:], ACT.Abs)
        nc.scalar.activation(identity[:], distance[:], ACT.Relu, bias=1.0, scale=-1.0)

        q_rows = qT[0].rearrange("(o p j) q -> o p j q", o=PASSES, j=PACK)
        nc.sync.dma_start(scale_pool[SCALES_FROM:P, :].bitcast(I32), k_scales.bitcast(I32).rearrange("o f t -> f o t"))
        nc.sync.dma_start(offsets[:], offs)
        nc.sync.dma_start(key_pool[:], k_words[0].rearrange("p t b -> p (t b)").bitcast(I32))
        for o in range(PASSES):
            nc.sync.dma_start(q_raw[o][:], q_rows[o])
        nc.sync.dma_start(v_pools[0][:, 0:V_AHEAD], vT[0:P, 0:V_AHEAD])

        listed_scales = sb.tile([P, N], U8, name="listed_scales", align_bytes=256)
        nc.vector.tensor_copy(listed_scales[:], scale_pool[:].indirect(offsets[:]))
        for a in range(4):
            rows = slice(SCALES_FROM + 8 * a, SCALES_FROM + 8 * a + 8)
            nc.sync.dma_start(key_scales[32 * a : 32 * a + 4, :, :].bitcast(I32), listed_scales[rows, :].bitcast(I32))
        nc.sync.dma_start(v_pools[0][:, V_AHEAD:T], vT[0:P, V_AHEAD:T])
        nc.sync.dma_start(v_pools[1][:], vT[P:DV, :])

        vs_listed = sb.tile([P, N], F32, name="vs_listed", align_bytes=256)
        vs_turned = banks.tile([P, PACK, P], F32, name="vs_turned", offset=BANK)
        vs_slot = placed.tile([P, PACK], F32, name="vs_slot", align_bytes=256, offset=VS_SLOT_AT)
        nc.scalar.activation(vs_listed[:], vs_pool[:].indirect(offsets[:]), ACT.Copy)
        vs_dealt = sb.tile([P, 2, N // 2], F32, name="vs_dealt", align_bytes=256)
        nc.scalar.copy(vs_dealt[:].rearrange("p u (b s) -> p u b s", s=RUN), vs_listed[:].rearrange("p (b u s) -> p u b s", u=2, s=RUN))
        for t in range(PACK):
            nc.tensor.transpose(vs_turned[:, t, :], vs_dealt[:, t // 2, t % 2 : N // 2 : 2], identity[:])

        q_bf = [placed.tile([P, NQ, PACK], BF16, name=f"q_bf{o}", align_bytes=256, offset=VS_AT + 1024 * o) for o in range(PASSES)]
        q_codes = [
            sb.tile([P, NQ], U32, name="q_codes0", align_bytes=256),
            placed.tile([P, NQ], U32, name="q_codes1", align_bytes=256, offset=QC1_AT),
        ]
        q_scales = [sb.tile([P, NQ], U8, name=f"q_scales{o}", align_bytes=256) for o in range(PASSES)]
        for o in range(PASSES):
            nc.scalar.activation(
                q_bf[o][:].rearrange("p (c i) j -> p c j i", i=4),
                q_raw[o][:].rearrange("p j (c i) -> p c j i", i=4),
                ACT.Copy,
            )
        nc.scalar.activation(vs_slot[:], vs_turned[:, :, VS_ROW], ACT.Copy)

        def quantise_queries(o):
            nc.vector.quantize_mx(q_codes[o][:].bitcast(FP8X4), q_scales[o][:], q_bf[o][:].rearrange("p q j -> p (q j)"))

        key_pairs = sb.tile([P, N], U32, name="key_pairs", align_bytes=256)
        key_words = [placed.tile([P, 2 * N], U8, name=f"key_words{o}", align_bytes=256, offset=at) for o, at in enumerate((Q0_AT, Q1_AT))]
        nc.vector.tensor_copy(key_pairs[:], key_pool[:].bitcast(U32).indirect(offsets[:]))
        halves = key_pairs[:].bitcast(U16).rearrange("p (i o) -> p o i", o=PASSES)
        quantise_queries(0)
        for o in range(PASSES):
            nc.vector.tensor_copy(key_words[o][:].bitcast(U16), halves[:, o, :])
        quantise_queries(1)

        scores = banks.tile([P, N], F32, name="scores", offset=0)
        for o in range(PASSES):
            nc.tensor.matmul_mx(
                scores[:],
                lhsT=q_codes[o][:].bitcast(FP8X4),
                lhsT_scale=q_scales[o][:],
                rhs=key_words[o][:].bitcast(FP4X4),
                rhs_scale=key_scales[:, o, :],
                start=(o == 0),
                stop=(o == PASSES - 1),
            )

        neg_max = placed.tile([P, 1], F32, name="neg_max", align_bytes=256, offset=MAX_AT)
        part_total = sb.tile([P, PACK], F32, name="part_total")
        total = sb.tile([P, 1], F32, name="total")
        probs = sb.tile([P, PACK, P], F32, name="probs", align_bytes=256)
        v_listed = [
            placed.tile([P, N], BF16, name="v_listed0", align_bytes=256, offset=QC1_AT),
            placed.tile([P, N], BF16, name="v_listed1", align_bytes=256, offset=MAX_AT),
        ]
        nc.vector.tensor_reduce(neg_max[:], scores[:], AXIS.X, ALU.max, negate=True)
        v_dealt = [tile[:].rearrange("p (u b s) -> p b u s", u=2, s=RUN) for tile in v_listed]

        def gather_values(h):
            cut = ON_VECTOR[h] // 16
            nc.vector.tensor_copy(v_dealt[h][:, 0 : cut // 2], v_pools[h][:].indirect(offsets[:, 0:cut]))
            nc.scalar.activation(v_dealt[h][:, cut // 2 : N // 32], v_pools[h][:].indirect(offsets[:, cut : N // 16]), ACT.Copy)

        gather_values(0)
        probs_turned = ps.tile([P, PACK, NQ], F32, name="probs_turned")
        score_planes = scores[:].rearrange("q (b u j e) -> q u e b j", u=2, j=RUN // 2, e=2)
        prob_planes = probs[:].rearrange("q (u e) (b j) -> q u e b j", u=2, j=RUN // 2)
        for t in range(PACK):
            u, e = divmod(t, 2)
            nc.scalar.activation(prob_planes[:, u, e], score_planes[:, u, e], ACT.Exp, bias=neg_max[:], accum_out=part_total[:, t : t + 1])
        nc.vector.tensor_reduce(total[:], part_total[:], AXIS.X, ALU.add)
        gather_values(1)

        v_codes = [sb.tile([P, P], U32, name=f"v_codes{h}", align_bytes=256) for h in range(V_BLOCKS)]
        inv_total = placed.tile([P, 1], F32, name="inv_total", align_bytes=256, offset=VS_SLOT_AT)
        v_scales = [sb.tile([P, P], U8, name=f"v_scales{h}", align_bytes=256) for h in range(V_BLOCKS)]
        v_bf = [sb.tile([P, P, PACK], BF16, name=f"v_bf{h}", align_bytes=256) for h in range(V_BLOCKS)]

        def turn_values(h, parts):
            v_turned = banks.tile([P, 2, P], F32, name=f"v_turned{h}", offset=BANK * h)
            words = v_listed[h][:].bitcast(F32)
            for u in range(2):
                nc.tensor.transpose(v_turned[:, u, :], words[:, u * P : (u + 1) * P], identity[:])
            for part in parts:
                nc.scalar.copy(v_bf[h][:, part, :].bitcast(F32), v_turned[:, :, part].rearrange("p u e -> p e u"))

        def quantise_values(h, parts):
            for part in parts:
                nc.vector.quantize_mx(
                    v_codes[h][:, part].bitcast(FP8X4), v_scales[h][:, part], v_bf[h][:, part, :].rearrange("p e t -> p (e t)")
                )

        whole, halved = [slice(0, P)], [slice(0, P // 2), slice(P // 2, P)]
        for t in range(PACK):
            nc.tensor.transpose(probs_turned[:, t, :], probs[:, t, :], identity[:])
        turn_values(0, whole)

        w_bf = sb.tile([P, NQ, PACK], BF16, name="w_bf", align_bytes=256)
        w_codes = sb.tile([P, NQ], U32, name="w_codes", align_bytes=256)
        w_scales = sb.tile([P, NQ], U8, name="w_scales", align_bytes=256)
        nc.vector.tensor_tensor(
            w_bf[:],
            probs_turned[:].rearrange("p t q -> p q t"),
            vs_slot[:].unsqueeze(1).to_broadcast([P, NQ, PACK]),
            ALU.mult,
        )
        turn_values(1, halved)
        quantise_values(0, whole)
        nc.vector.quantize_mx(w_codes[:].bitcast(FP8X4), w_scales[:], w_bf[:].rearrange("p q t -> p (q t)"))
        nc.vector.reciprocal(inv_total[:], total[:])
        quantise_values(1, halved)

        for h, parts in enumerate((whole, halved)):
            result = sb.tile([P, P], F32, name=f"result{h}", align_bytes=256)
            for part in parts:
                sums = ps.tile([P, part.stop - part.start], F32, name=f"sums{h}_{part.start}")
                nc.tensor.matmul_mx(
                    sums[:],
                    lhsT=w_codes[:].bitcast(FP8X4),
                    lhsT_scale=w_scales[:],
                    rhs=v_codes[h][:, part].bitcast(FP8X4),
                    rhs_scale=v_scales[h][:, part],
                    start=True,
                    stop=True,
                )
                if h == 1 and part.stop == P:
                    nc.vector.tensor_scalar(result[:, part], sums[:], inv_total[:], None, ALU.mult)
                else:
                    nc.scalar.activation(result[:, part], sums[:], ACT.Copy, scale=inv_total[:])
            nc.sync.dma_start(out[0][:, h * P : (h + 1) * P], result[:])
